import numpy as np
import ml_dtypes


def mxq(x, axis, fmt="e4m3"):
    dtype, down = {"e4m3": (ml_dtypes.float8_e4m3fn, 7), "e5m2": (ml_dtypes.float8_e5m2, 14)}[fmt]
    v = np.moveaxis(np.asarray(x, np.float32).astype(ml_dtypes.bfloat16).astype(np.float64), axis, -1)
    blocks = v.reshape(v.shape[:-1] + (-1, 32))
    amax = np.abs(blocks).max(-1, keepdims=True)
    byte = np.maximum(np.where(amax > 0, np.frexp(amax)[1] - 1 + 127, 0) - down, 1)
    scale = np.exp2(byte - 127.0)
    codes = (blocks / scale).astype(np.float32).astype(dtype).astype(np.float64)
    return np.moveaxis((codes * scale).reshape(v.shape), -1, axis)


WIDE = False


def mx_kscale(k):
    if not WIDE:
        return np.ones(k)
    levels = np.array([10, -10, 5, -5, 0])
    if k % 512:
        return np.exp2(np.random.permutation(np.resize(levels, k // 32))).repeat(32)
    a = np.empty((k // 512, 16))
    for p in range(k // 512):
        a[p, :8] = np.random.permutation(np.resize(levels, 8))
        for g in range(8):
            far = levels[np.abs(levels - a[p, g]) >= 10]
            a[p, g + 8] = far[np.random.randint(len(far))]
    return np.exp2(a.ravel()).repeat(32)


def f64(x):
    return np.asarray(x).astype(np.float64)


def striped(idx):
    return np.tile(idx.reshape(-1, 16).T, (8, 1)).astype(np.uint16)


def unstriped(offs):
    return offs[:16].T.reshape(-1).astype(np.int64)


def striped8(idx):
    return np.concatenate([x.reshape(-1, 16).T for x in idx]).astype(np.uint16)


def runs(offs, k):
    lists = np.stack([offs[16 * r : 16 * r + 16].T.reshape(-1) for r in range(8)]).astype(np.int64)
    return lists[np.arange(k) % 512 // 64]


def pack_weight(w):
    k, n = w.shape
    w = f64(np.asarray(w, np.float32).astype(ml_dtypes.bfloat16)).reshape(k // 32, 32, n)
    amax = np.abs(w).max(1)
    byte = np.clip(np.where(amax > 0, np.frexp(amax)[1] - 1 + 127 - 7, 1), 1, 254)
    scaled = (w * np.exp2(127.0 - byte)[:, None, :]).reshape(k, n).astype(np.float32)
    words = np.ascontiguousarray(scaled.reshape(k // 512, 128, 4, n).transpose(0, 1, 3, 2)).astype(ml_dtypes.float8_e4m3fn).view(np.uint8)
    return words, np.ascontiguousarray(byte.astype(np.uint8).reshape(k // 512, 16, n))


def unpack_weight(words, scales):
    g, p, n, _ = words.shape
    vals = np.ascontiguousarray(words).view(ml_dtypes.float8_e4m3fn).astype(np.float64) * np.repeat(np.exp2(scales.astype(np.float64) - 127.0), 8, axis=1)[..., None]
    return vals.transpose(0, 1, 3, 2).reshape(g * 512, n)


def gelu(v):
    return 0.5 * v * (1.0 + np.tanh(np.sqrt(2.0 / np.pi) * (v + 0.044715 * v**3)))

def planes(y):
    n, m = y.shape
    v = y.astype(np.float32).astype(ml_dtypes.bfloat16).astype(np.float64).reshape(n // 32, 32, m)
    top = np.abs(v).max(1)
    byte = np.clip(np.where(top > 0, np.frexp(top)[1] - 1 + 127 - 7, 1), 1, 254)
    codes = (v * np.exp2(127.0 - byte)[:, None, :]).reshape(n, m).astype(np.float32).astype(ml_dtypes.float8_e4m3fn).view(np.uint8)
    words = codes.reshape(n // 512, 128, 4, m).transpose(0, 1, 3, 2)
    return np.ascontiguousarray(words), np.ascontiguousarray(byte.astype(np.uint8).reshape(n // 512, 16, m))


K, T, S, N, H, U = 512, 2048, 512, 512, 512, 512


def setup_inputs():
    n = np.random.standard_normal
    s = mx_kscale(K)[:, None]
    u = mx_kscale(H)
    packed_xT = pack_weight(n((K, T)) * s)
    packed_w3 = pack_weight(n((H, N)) / np.sqrt(H) / u[:, None])
    packed_w4 = pack_weight(n((H, N)) / np.sqrt(H) / u[:, None])
    return {
        "x_words": packed_xT[0],
        "x_scales": packed_xT[1],
        "w1": (n((K, H)) / np.sqrt(K) / s * u).astype(np.float32),
        "w2": (n((K, H)) / np.sqrt(K) / s * u).astype(np.float32),
        "w3_words": packed_w3[0],
        "w3_scales": packed_w3[1],
        "w4_words": packed_w4[0],
        "w4_scales": packed_w4[1],
        "mix": np.random.uniform(0.0, 1.0, (N, U)).astype(np.float32),
        "offs": striped(np.random.permutation(T)[:S]),
        "task": striped8(np.random.randint(0, U, (8, S))),
    }


def reference(x_words, x_scales, w1, w2, w3_words, w3_scales, w4_words, w4_scales, mix, offs, task):
    xq = unpack_weight(x_words, x_scales)[:, unstriped(offs)]
    z2 = gelu(mxq(f64(w2), 0, "e4m3").T @ xq)
    b = unpack_weight(w4_words, w4_scales).T @ mxq(z2, 0, "e4m3")
    q = f64(mix)[np.arange(N)[:, None], runs(task, N)]
    z = gelu(mxq(f64(w1), 0, "e4m3").T @ xq)
    a = unpack_weight(w3_words, w3_scales).T @ mxq(z, 0, "e4m3")
    out_0 = b + q * (a - b)
    return (out_0,) + planes(out_0)

@@ -1,0 +1,253 @@
+from contextlib import ExitStack
+
+import concourse.mybir as mybir
+
+K, T, S, N, H, U = 512, 2048, 512, 512, 512, 512
+FLOPS = 4 * 2 * 512 * 512 * 512
+
+F32 = mybir.dt.float32
+BF16 = mybir.dt.bfloat16
+I32 = mybir.dt.int32
+U32 = mybir.dt.uint32
+U16 = mybir.dt.uint16
+U8 = mybir.dt.uint8
+FP8X4 = mybir.dt.float8_e4m3fn_x4
+ALU = mybir.AluOpType
+ACT = mybir.ActivationFunctionType
+
+P = 128
+PACK = 4
+CH = 128
+NCH = S // CH
+HALF = 256
+
+
+def tile_picked_expertpair_gelu_po_kernel(
+    tc, x_words, x_scales, w1, w2, w3_words, w3_scales, w4_words, w4_scales, mix, offs, task, out_0, out_1, out_2
+):
+    nc = tc.nc
+    with ExitStack() as ctx:
+        keep = ctx.enter_context(tc.tile_pool(name="keep", bufs=1))
+        ring = ctx.enter_context(tc.tile_pool(name="ring", bufs=2))
+        psum = ctx.enter_context(tc.psum_pool(name="psum", bufs=1))
+
+        offs_t = keep.tile([P, S // 16], U16, name="offs_t")
+        task_t = keep.tile([P, S // 16], U16, name="task_t")
+        xw = keep.tile([P, T], I32, name="xw", align_bytes=64)
+        xs = keep.tile([P, T], U8, name="xs", align_bytes=64)
+        ws_raw = keep.tile([P, N], U8, name="ws_raw", align_bytes=64)
+        ww_raw = keep.tile([P, 2, N], I32, name="ww_raw", align_bytes=64)
+        mix_t = [keep.tile([P, U], F32, name="mix%d" % t, align_bytes=64) for t in range(PACK)]
+        w_raw = {(n, h): keep.tile([P, PACK, HALF], F32, name="w_raw%d%d" % (n, h), align_bytes=64) for n in (1, 2) for h in range(2)}
+        warm = keep.tile([P, 1], F32, name="warm")
+        warm2 = keep.tile([P, 1], F32, name="warm2")
+
+        nc.gpsimd.memset(xs[:].bitcast(I32), 0)
+        nc.vector.memset(ws_raw[:].bitcast(I32), 0)
+        nc.vector.memset(warm[:], 0.0)
+
+        nc.sync.dma_start(task_t[:], task)
+        mix_rows = mix.rearrange("(p t) u -> p t u", t=PACK)
+        w_rows = {1: w1.rearrange("(p j) c -> p j c", j=PACK), 2: w2.rearrange("(p j) c -> p j c", j=PACK)}
+
+        def load_mix(t):
+            nc.sync.dma_start(mix_t[t][:], mix_rows[:, t, :])
+
+        def load_w(n, h):
+            nc.sync.dma_start(w_raw[n, h][:], w_rows[n][:, :, h * HALF : (h + 1) * HALF])
+
+        load_mix(0)
+        nc.sync.dma_start(offs_t[:], offs)
+        for q in range(4):
+            nc.scalar.dma_start(xs[32 * q : 32 * q + 4, :].bitcast(I32), x_scales[0, 4 * q : 4 * q + 4, :].bitcast(I32))
+        nc.scalar.activation(warm2[:], warm[:], ACT.Gelu_apprx_tanh)
+
+        def load_ws(i, q):
+            sc = (w3_scales, w4_scales)[i]
+            nc.sync.dma_start(
+                ws_raw[32 * q + 4 * i : 32 * q + 4 * i + 4, :].bitcast(I32), sc[0, 4 * q : 4 * q + 4, :].bitcast(I32)
+            )
+
+        load_mix(1)
+        load_w(2, 0)
+        load_w(2, 1)
+        load_ws(0, 0)
+        nc.sync.dma_start(xw[:], x_words[0].rearrange("p n t -> p (n t)").bitcast(I32))
+        load_ws(0, 1)
+        load_ws(0, 2)
+        load_mix(2)
+        load_ws(0, 3)
+        load_w(1, 0)
+        load_ws(1, 0)
+        load_w(1, 1)
+        load_ws(1, 1)
+        load_ws(1, 2)
+        nc.sync.dma_start(ww_raw[:, 1, :], w4_words[0].rearrange("p n t -> p (n t)").bitcast(I32))
+        load_ws(1, 3)
+        nc.sync.dma_start(ww_raw[:, 0, :], w3_words[0].rearrange("p n t -> p (n t)").bitcast(I32))
+        load_mix(3)
+
+        q4 = keep.tile([P, PACK, S], F32, name="q4", align_bytes=64)
+
+        def gather_q(t):
+            for h in range(2):
+                nc.vector.tensor_copy(
+                    q4[:, t, h * HALF : (h + 1) * HALF], mix_t[t][:].indirect(task_t[:, h * 16 : (h + 1) * 16])
+                )
+
+        xg_w = keep.tile([P, S], U32, name="xg_w", align_bytes=64)
+        xg_s = keep.tile([P, S], U8, name="xg_s", align_bytes=64)
+        w_bf = {n: keep.tile([P, PACK * H], BF16, name="w_bf%d" % n, align_bytes=64) for n in (1, 2)}
+        w_c = {n: keep.tile([P, H], U32, name="w_c%d" % n, align_bytes=64) for n in (1, 2)}
+        w_s = {n: keep.tile([P, H], U8, name="w_s%d" % n, align_bytes=64) for n in (1, 2)}
+
+        def cast_w(n, h):
+            dst = w_bf[n][:].rearrange("p (t m j) -> p m j t", t=PACK, j=PACK)[:, h * 64 : (h + 1) * 64]
+            src = w_raw[n, h][:].rearrange("p j (m t) -> p m j t", t=PACK)
+            nc.scalar.copy(dst, src)
+
+        def quant_w(n):
+            nc.vector.quantize_mx(out=w_c[n][:].bitcast(FP8X4), scales=w_s[n][:], in_=w_bf[n][:])
+
+        z_c = {n: keep.tile([P, S], U32, name="z_c%d" % n, align_bytes=64) for n in (1, 2)}
+        z_s = {n: keep.tile([P, S], U8, name="z_s%d" % n, align_bytes=64) for n in (1, 2)}
+        z_bf = {}
+
+        def layer1(n, c):
+            cols = slice(c * CH, (c + 1) * CH)
+            bank = psum.tile([P, PACK, CH], F32, name="hid", tag="hid", bufs=2)
+            for t in range(PACK):
+                tc_ = slice(t * P, (t + 1) * P)
+                nc.tensor.matmul_mx(
+                    out=bank[:, t, :],
+                    lhsT=w_c[n][:, tc_].bitcast(FP8X4),
+                    lhsT_scale=w_s[n][:, tc_],
+                    rhs=xg_w[:, cols].bitcast(FP8X4),
+                    rhs_scale=xg_s[:, cols],
+                    start=True,
+                    stop=True,
+                )
+            z_bf[n, c] = keep.tile([P, CH * PACK], BF16, name="z_bf%d%d" % (n, c), align_bytes=64)
+            nc.scalar.activation(
+                z_bf[n, c][:].rearrange("p (s t) -> p s t", t=PACK), bank[:].rearrange("p t s -> p s t"), ACT.Gelu_apprx_tanh
+            )
+
+        def quant_z(n, c, src):
+            cols = slice(c * CH, (c + 1) * CH)
+            nc.vector.quantize_mx(out=z_c[n][:, cols].bitcast(FP8X4), scales=z_s[n][:, cols], in_=src)
+
+        nz = {}
+
+        def negate(c):
+            nz[c] = keep.tile([P, CH * PACK], BF16, name="nz%d" % c, align_bytes=64)
+            nc.vector.tensor_scalar_mul(nz[c][:], z_bf[2, c][:], -1.0)
+
+        ww = keep.tile([P, 2, N], U32, name="ww", align_bytes=64)
+        ws = keep.tile([P, N], U8, name="ws", align_bytes=64)
+
+        def deal():
+            nc.vector.tensor_copy(ws[:].rearrange("p (t m) -> p t m", t=PACK), ws_raw[:].rearrange("p (m t) -> p t m", t=PACK))
+            nc.vector.tensor_copy(
+                ww[:].rearrange("p w (t m) -> p w m t", t=PACK),
+                ww_raw[:].bitcast(U32).rearrange("p w (m t) -> p w m t", t=PACK),
+            )
+
+        def pass2(bank, t, c, n, start, stop):
+            cols = slice(c * CH, (c + 1) * CH)
+            tc_ = slice(t * P, (t + 1) * P)
+            i = n - 1
+            nc.tensor.matmul_mx(
+                out=bank[:, t, :],
+                lhsT=ww[:, i, tc_].bitcast(FP8X4),
+                lhsT_scale=ws[4 * i : P, tc_],
+                rhs=z_c[n][:, cols].bitcast(FP8X4),
+                rhs_scale=z_s[n][:, cols],
+                start=start,
+                stop=stop,
+            )
+
+        nb = {}
+
+        def layer2_b(c):
+            nb[c] = psum.tile([P, PACK, CH], F32, name="nb%d" % c, tag="nb%d" % c)
+            for t in range(PACK):
+                pass2(nb[c], t, c, 2, True, True)
+
+        diff = {}
+
+        def layer2_d(c):
+            diff[c] = psum.tile([P, PACK, CH], F32, name="diff", tag="diff", bufs=2)
+            for t in range(PACK):
+                pass2(diff[c], t, c, 1, True, False)
+                pass2(diff[c], t, c, 2, False, True)
+
+        o_c = keep.tile([P, S], I32, name="o_c", align_bytes=64)
+        o_s = keep.tile([P, S], U8, name="o_s", align_bytes=64)
+        out_rows = out_0.rearrange("(p t) s -> p t s", t=PACK)
+        o1 = out_1[0].rearrange("p n t -> p (n t)").bitcast(I32)
+        prod = {}
+        y = {}
+        y_bf = {}
+
+        def mul(c):
+            cols = slice(c * CH, (c + 1) * CH)
+            prod[c] = ring.tile([P, PACK, CH], F32, name="prod", tag="prod")
+            nc.vector.tensor_tensor(prod[c][:], diff[c][:], q4[:, :, cols], ALU.mult)
+
+        def sub(c):
+            cols = slice(c * CH, (c + 1) * CH)
+            y[c] = keep.tile([P, PACK, CH], F32, name="y%d" % c, align_bytes=64)
+            nc.vector.tensor_tensor(y[c][:], prod[c][:], nb[c][:], ALU.subtract)
+            nc.sync.dma_start(out_rows[:, :, cols], y[c][:])
+            y_bf[c] = keep.tile([P, CH * PACK], BF16, name="y_bf%d" % c, align_bytes=64)
+            nc.scalar.copy(
+                y_bf[c][:].rearrange("p (g i t) -> p g t i", i=4, t=PACK), y[c][:].rearrange("p t (g i) -> p g t i", i=4)
+            )
+
+        def quant_y(c):
+            cols = slice(c * CH, (c + 1) * CH)
+            nc.vector.quantize_mx(out=o_c[:, cols].bitcast(FP8X4), scales=o_s[:, cols], in_=y_bf[c][:])
+
+        gather_q(0)
+        gather_q(1)
+        cast_w(2, 0)
+        cast_w(2, 1)
+        nc.vector.tensor_copy(xg_s[:], xs[:].indirect(offs_t[:]))
+        quant_w(2)
+        for h in range(2):
+            nc.vector.tensor_copy(
+                xg_w[:, h * HALF : (h + 1) * HALF], xw[:].bitcast(U32).indirect(offs_t[:, h * 16 : (h + 1) * 16])
+            )
+        layer1(2, 0)
+        layer1(2, 1)
+        cast_w(1, 0)
+        cast_w(1, 1)
+        quant_w(1)
+        layer1(2, 2)
+        layer1(2, 3)
+        gather_q(2)
+        deal()
+        for c in range(NCH):
+            negate(c)
+        for c in range(NCH):
+            quant_z(2, c, nz[c][:])
+        for c in range(NCH):
+            layer1(1, c)
+        for c in range(NCH):
+            layer2_b(c)
+        gather_q(3)
+        for c in range(NCH + 2):
+            if c < NCH:
+                quant_z(1, c, z_bf[1, c][:])
+                layer2_d(c)
+            if 1 <= c <= NCH:
+                mul(c - 1)
+            if c >= 2:
+                quant_y(c - 2)
+            if 1 <= c <= NCH:
+                sub(c - 1)
+        for h in range(2):
+            nc.sync.dma_start(o1[:, h * HALF : (h + 1) * HALF], o_c[:, h * HALF : (h + 1) * HALF])
+        for q in range(4):
+            eng = nc.scalar if q % 2 else nc.sync
+            eng.dma_start(out_2[0, 4 * q : 4 * q + 4, :].bitcast(I32), o_s[32 * q : 32 * q + 4, :].bitcast(I32))

@@ -36,15 +36,16 @@ def tile_picked_expertpair_gelu_po_kernel(
         xw = keep.tile([P, T], I32, name="xw", align_bytes=64)
         xs = keep.tile([P, T], U8, name="xs", align_bytes=64)
         ws_raw = keep.tile([P, N], U8, name="ws_raw", align_bytes=64)
-        ww_raw = keep.tile([P, 2, N], I32, name="ww_raw", align_bytes=64)
+        ww_raw = keep.tile([P, 2, N], I32, name="ww_raw", tag="ww_raw", align_bytes=64)
         mix_t = [keep.tile([P, U], F32, name="mix%d" % t, align_bytes=64) for t in range(PACK)]
-        w_raw = {(n, h): keep.tile([P, PACK, HALF], F32, name="w_raw%d%d" % (n, h), align_bytes=64) for n in (1, 2) for h in range(2)}
+        w_raw = {(1, h): keep.tile([P, PACK, HALF], F32, name="w_raw1%d" % h, tag="w_raw1%d" % h, align_bytes=64) for h in range(2)}
+        w2_raw = keep.tile([P, PACK, H], F32, name="w2_raw", align_bytes=64)
         warm = keep.tile([P, 1], F32, name="warm")
         warm2 = keep.tile([P, 1], F32, name="warm2")
 
         nc.gpsimd.memset(xs[:].bitcast(I32), 0)
-        nc.vector.memset(ws_raw[:].bitcast(I32), 0)
-        nc.vector.memset(warm[:], 0.0)
+        nc.gpsimd.memset(ws_raw[:].bitcast(I32), 0)
+        nc.gpsimd.memset(warm[:], 0.0)
 
         nc.sync.dma_start(task_t[:], task)
         mix_rows = mix.rearrange("(p t) u -> p t u", t=PACK)
@@ -57,35 +58,24 @@ def tile_picked_expertpair_gelu_po_kernel(
             nc.sync.dma_start(w_raw[n, h][:], w_rows[n][:, :, h * HALF : (h + 1) * HALF])
 
         load_mix(0)
-        nc.sync.dma_start(offs_t[:], offs)
         for q in range(4):
-            nc.scalar.dma_start(xs[32 * q : 32 * q + 4, :].bitcast(I32), x_scales[0, 4 * q : 4 * q + 4, :].bitcast(I32))
+            nc.sync.dma_start(xs[32 * q : 32 * q + 4, :].bitcast(I32), x_scales[0, 4 * q : 4 * q + 4, :].bitcast(I32))
         nc.scalar.activation(warm2[:], warm[:], ACT.Gelu_apprx_tanh)
-
-        def load_ws(i, q):
-            sc = (w3_scales, w4_scales)[i]
-            nc.sync.dma_start(
-                ws_raw[32 * q + 4 * i : 32 * q + 4 * i + 4, :].bitcast(I32), sc[0, 4 * q : 4 * q + 4, :].bitcast(I32)
-            )
-
+        for i, sc in enumerate((w3_scales, w4_scales)):
+            for q in range(4):
+                nc.gpsimd.dma_start(
+                    ws_raw[32 * q + 4 * i : 32 * q + 4 * i + 4, :].bitcast(I32), sc[0, 4 * q : 4 * q + 4, :].bitcast(I32)
+                )
         load_mix(1)
-        load_w(2, 0)
-        load_w(2, 1)
-        load_ws(0, 0)
-        nc.sync.dma_start(xw[:], x_words[0].rearrange("p n t -> p (n t)").bitcast(I32))
-        load_ws(0, 1)
-        load_ws(0, 2)
+        nc.sync.dma_start(w2_raw[:], w_rows[2])
+        nc.sync.dma_start(offs_t[:], offs)
         load_mix(2)
-        load_ws(0, 3)
+        nc.sync.dma_start(xw[:], x_words[0].rearrange("p n t -> p (n t)").bitcast(I32))
         load_w(1, 0)
-        load_ws(1, 0)
-        load_w(1, 1)
-        load_ws(1, 1)
-        load_ws(1, 2)
-        nc.sync.dma_start(ww_raw[:, 1, :], w4_words[0].rearrange("p n t -> p (n t)").bitcast(I32))
-        load_ws(1, 3)
-        nc.sync.dma_start(ww_raw[:, 0, :], w3_words[0].rearrange("p n t -> p (n t)").bitcast(I32))
         load_mix(3)
+        load_w(1, 1)
+        nc.sync.dma_start(ww_raw[:, 1, :], w4_words[0].rearrange("p n t -> p (n t)").bitcast(I32))
+        nc.sync.dma_start(ww_raw[:, 0, :], w3_words[0].rearrange("p n t -> p (n t)").bitcast(I32))
 
         q4 = keep.tile([P, PACK, S], F32, name="q4", align_bytes=64)
 
@@ -103,8 +93,12 @@ def tile_picked_expertpair_gelu_po_kernel(
 
         def cast_w(n, h):
             dst = w_bf[n][:].rearrange("p (t m j) -> p m j t", t=PACK, j=PACK)[:, h * 64 : (h + 1) * 64]
-            src = w_raw[n, h][:].rearrange("p j (m t) -> p m j t", t=PACK)
-            nc.scalar.copy(dst, src)
+            raw = w_raw[n, h][:] if n == 1 else w2_raw[:, :, h * HALF : (h + 1) * HALF]
+            src = raw.rearrange("p j (m t) -> p m j t", t=PACK)
+            if (n, h) == (1, 1):
+                nc.vector.tensor_copy(dst, src)
+            else:
+                nc.scalar.copy(dst, src)
 
         def quant_w(n):
             nc.vector.quantize_mx(out=w_c[n][:].bitcast(FP8X4), scales=w_s[n][:], in_=w_bf[n][:])
@@ -112,10 +106,11 @@ def tile_picked_expertpair_gelu_po_kernel(
         z_c = {n: keep.tile([P, S], U32, name="z_c%d" % n, align_bytes=64) for n in (1, 2)}
         z_s = {n: keep.tile([P, S], U8, name="z_s%d" % n, align_bytes=64) for n in (1, 2)}
         z_bf = {}
+        z_all = {}
 
         def layer1(n, c):
             cols = slice(c * CH, (c + 1) * CH)
-            bank = psum.tile([P, PACK, CH], F32, name="hid", tag="hid", bufs=2)
+            bank = psum.tile([P, PACK, CH], F32, name="hid", tag="bank", bufs=8)
             for t in range(PACK):
                 tc_ = slice(t * P, (t + 1) * P)
                 nc.tensor.matmul_mx(
@@ -127,9 +122,11 @@ def tile_picked_expertpair_gelu_po_kernel(
                     start=True,
                     stop=True,
                 )
-            z_bf[n, c] = keep.tile([P, CH * PACK], BF16, name="z_bf%d%d" % (n, c), align_bytes=64)
+            if c == 0:
+                z_all[n] = keep.tile([P, S * PACK], BF16, name="z_bf%d" % n, tag="w_raw10" if n == 2 else "z_bf1", align_bytes=64)
+            z_bf[n, c] = z_all[n][:, c * CH * PACK : (c + 1) * CH * PACK]
             nc.scalar.activation(
-                z_bf[n, c][:].rearrange("p (s t) -> p s t", t=PACK), bank[:].rearrange("p t s -> p s t"), ACT.Gelu_apprx_tanh
+                z_bf[n, c].rearrange("p (s t) -> p s t", t=PACK), bank[:].rearrange("p t s -> p s t"), ACT.Gelu_apprx_tanh
             )
 
         def quant_z(n, c, src):
@@ -140,17 +137,19 @@ def tile_picked_expertpair_gelu_po_kernel(
 
         def negate(c):
             nz[c] = keep.tile([P, CH * PACK], BF16, name="nz%d" % c, align_bytes=64)
-            nc.vector.tensor_scalar_mul(nz[c][:], z_bf[2, c][:], -1.0)
+            nc.vector.tensor_scalar_mul(nz[c][:], z_bf[2, c], -1.0)
 
         ww = keep.tile([P, 2, N], U32, name="ww", align_bytes=64)
-        ws = keep.tile([P, N], U8, name="ws", align_bytes=64)
+        dealt = {}
 
         def deal():
-            nc.vector.tensor_copy(ws[:].rearrange("p (t m) -> p t m", t=PACK), ws_raw[:].rearrange("p (m t) -> p t m", t=PACK))
             nc.vector.tensor_copy(
                 ww[:].rearrange("p w (t m) -> p w m t", t=PACK),
                 ww_raw[:].bitcast(U32).rearrange("p w (m t) -> p w m t", t=PACK),
             )
+            ws = keep.tile([P, N], U8, name="ws", tag="ww_raw", align_bytes=64)
+            nc.vector.tensor_copy(ws[:].rearrange("p (t m) -> p t m", t=PACK), ws_raw[:].rearrange("p (m t) -> p t m", t=PACK))
+            dealt["ws"] = ws
 
         def pass2(bank, t, c, n, start, stop):
             cols = slice(c * CH, (c + 1) * CH)
@@ -159,7 +158,7 @@ def tile_picked_expertpair_gelu_po_kernel(
             nc.tensor.matmul_mx(
                 out=bank[:, t, :],
                 lhsT=ww[:, i, tc_].bitcast(FP8X4),
-                lhsT_scale=ws[4 * i : P, tc_],
+                lhsT_scale=dealt["ws"][4 * i : P, tc_],
                 rhs=z_c[n][:, cols].bitcast(FP8X4),
                 rhs_scale=z_s[n][:, cols],
                 start=start,
@@ -169,14 +168,14 @@ def tile_picked_expertpair_gelu_po_kernel(
         nb = {}
 
         def layer2_b(c):
-            nb[c] = psum.tile([P, PACK, CH], F32, name="nb%d" % c, tag="nb%d" % c)
+            nb[c] = psum.tile([P, PACK, CH], F32, name="nb%d" % c, tag="bank", bufs=8)
             for t in range(PACK):
                 pass2(nb[c], t, c, 2, True, True)
 
         diff = {}
 
         def layer2_d(c):
-            diff[c] = psum.tile([P, PACK, CH], F32, name="diff", tag="diff", bufs=2)
+            diff[c] = psum.tile([P, PACK, CH], F32, name="diff", tag="bank", bufs=8)
             for t in range(PACK):
                 pass2(diff[c], t, c, 1, True, False)
                 pass2(diff[c], t, c, 2, False, True)
@@ -200,9 +199,13 @@ def tile_picked_expertpair_gelu_po_kernel(
             nc.vector.tensor_tensor(y[c][:], prod[c][:], nb[c][:], ALU.subtract)
             nc.sync.dma_start(out_rows[:, :, cols], y[c][:])
             y_bf[c] = keep.tile([P, CH * PACK], BF16, name="y_bf%d" % c, align_bytes=64)
-            nc.scalar.copy(
-                y_bf[c][:].rearrange("p (g i t) -> p g t i", i=4, t=PACK), y[c][:].rearrange("p t (g i) -> p g t i", i=4)
-            )
+            dst = y_bf[c][:].rearrange("p (g i t) -> p g t i", i=4, t=PACK)
+            src = y[c][:].rearrange("p t (g i) -> p g t i", i=4)
+            if c < NCH - 1:
+                nc.scalar.copy(dst, src)
+            else:
+                nc.scalar.copy(dst[:, :16], src[:, :16])
+                nc.vector.tensor_copy(dst[:, 16:], src[:, 16:])
 
         def quant_y(c):
             cols = slice(c * CH, (c + 1) * CH)
@@ -210,44 +213,48 @@ def tile_picked_expertpair_gelu_po_kernel(
 
         gather_q(0)
         gather_q(1)
-        cast_w(2, 0)
-        cast_w(2, 1)
+        gather_q(2)
         nc.vector.tensor_copy(xg_s[:], xs[:].indirect(offs_t[:]))
-        quant_w(2)
         for h in range(2):
             nc.vector.tensor_copy(
                 xg_w[:, h * HALF : (h + 1) * HALF], xw[:].bitcast(U32).indirect(offs_t[:, h * 16 : (h + 1) * 16])
             )
-        layer1(2, 0)
-        layer1(2, 1)
+        cast_w(2, 0)
+        cast_w(2, 1)
+        quant_w(2)
         cast_w(1, 0)
         cast_w(1, 1)
         quant_w(1)
-        layer1(2, 2)
-        layer1(2, 3)
-        gather_q(2)
+        for n, c in ((2, 0), (2, 1), (1, 0), (1, 1), (2, 2), (1, 2), (2, 3), (1, 3)):
+            layer1(n, c)
         deal()
-        for c in range(NCH):
+
+        def hidden(c):
             negate(c)
-        for c in range(NCH):
             quant_z(2, c, nz[c][:])
-        for c in range(NCH):
-            layer1(1, c)
-        for c in range(NCH):
-            layer2_b(c)
+            quant_z(1, c, z_bf[1, c])
+
+        hidden(0)
+        hidden(1)
         gather_q(3)
         for c in range(NCH + 2):
+            if c == 0:
+                layer2_d(0)
+                layer2_b(0)
+            if c + 1 < NCH:
+                layer2_d(c + 1)
+                layer2_b(c + 1)
+            if c + 2 < NCH:
+                hidden(c + 2)
             if c < NCH:
-                quant_z(1, c, z_bf[1, c][:])
-                layer2_d(c)
-            if 1 <= c <= NCH:
-                mul(c - 1)
+                mul(c)
             if c >= 2:
                 quant_y(c - 2)
-            if 1 <= c <= NCH:
-                sub(c - 1)
-        for h in range(2):
-            nc.sync.dma_start(o1[:, h * HALF : (h + 1) * HALF], o_c[:, h * HALF : (h + 1) * HALF])
+            if c < NCH:
+                sub(c)
+        last = S - CH
+        nc.sync.dma_start(o1[:, :last], o_c[:, :last])
+        nc.sync.dma_start(o1[:, last:], o_c[:, last:])
         for q in range(4):
             eng = nc.scalar if q % 2 else nc.sync
             eng.dma_start(out_2[0, 4 * q : 4 * q + 4, :].bitcast(I32), o_s[32 * q : 32 * q + 4, :].bitcast(I32))

@@ -43,9 +43,9 @@ def tile_picked_expertpair_gelu_po_kernel(
         warm = keep.tile([P, 1], F32, name="warm")
         warm2 = keep.tile([P, 1], F32, name="warm2")
 
-        nc.gpsimd.memset(xs[:].bitcast(I32), 0)
         nc.gpsimd.memset(ws_raw[:].bitcast(I32), 0)
-        nc.gpsimd.memset(warm[:], 0.0)
+        nc.vector.memset(xs[:].bitcast(I32), 0)
+        nc.vector.memset(warm[:], 0.0)
 
         nc.sync.dma_start(task_t[:], task)
         mix_rows = mix.rearrange("(p t) u -> p t u", t=PACK)
@@ -57,20 +57,32 @@ def tile_picked_expertpair_gelu_po_kernel(
         def load_w(n, h):
             nc.sync.dma_start(w_raw[n, h][:], w_rows[n][:, :, h * HALF : (h + 1) * HALF])
 
-        load_mix(0)
-        for q in range(4):
+        def load_xs(q):
             nc.sync.dma_start(xs[32 * q : 32 * q + 4, :].bitcast(I32), x_scales[0, 4 * q : 4 * q + 4, :].bitcast(I32))
+
+        def load_ws(eng, i, q):
+            sc = (w3_scales, w4_scales)[i]
+            eng.dma_start(
+                ws_raw[32 * q + 4 * i : 32 * q + 4 * i + 4, :].bitcast(I32), sc[0, 4 * q : 4 * q + 4, :].bitcast(I32)
+            )
+
+        load_mix(0)
         nc.scalar.activation(warm2[:], warm[:], ACT.Gelu_apprx_tanh)
-        for i, sc in enumerate((w3_scales, w4_scales)):
-            for q in range(4):
-                nc.gpsimd.dma_start(
-                    ws_raw[32 * q + 4 * i : 32 * q + 4 * i + 4, :].bitcast(I32), sc[0, 4 * q : 4 * q + 4, :].bitcast(I32)
-                )
+        for q in range(4):
+            load_ws(nc.gpsimd, 1, q)
         load_mix(1)
-        nc.sync.dma_start(w2_raw[:], w_rows[2])
         nc.sync.dma_start(offs_t[:], offs)
+        load_xs(0)
+        load_xs(1)
+        nc.sync.dma_start(w2_raw[:], w_rows[2])
+        load_xs(2)
+        load_xs(3)
         load_mix(2)
+        load_ws(nc.sync, 0, 0)
+        load_ws(nc.sync, 0, 1)
         nc.sync.dma_start(xw[:], x_words[0].rearrange("p n t -> p (n t)").bitcast(I32))
+        load_ws(nc.sync, 0, 2)
+        load_ws(nc.sync, 0, 3)
         load_w(1, 0)
         load_mix(3)
         load_w(1, 1)
@@ -87,7 +99,7 @@ def tile_picked_expertpair_gelu_po_kernel(
 
         xg_w = keep.tile([P, S], U32, name="xg_w", align_bytes=64)
         xg_s = keep.tile([P, S], U8, name="xg_s", align_bytes=64)
-        w_bf = {n: keep.tile([P, PACK * H], BF16, name="w_bf%d" % n, align_bytes=64) for n in (1, 2)}
+        w_bf = {n: keep.tile([P, PACK * H], BF16, name="w_bf%d" % n, tag="w_bf%d" % n, align_bytes=64) for n in (1, 2)}
         w_c = {n: keep.tile([P, H], U32, name="w_c%d" % n, align_bytes=64) for n in (1, 2)}
         w_s = {n: keep.tile([P, H], U8, name="w_s%d" % n, align_bytes=64) for n in (1, 2)}
 
@@ -96,12 +108,19 @@ def tile_picked_expertpair_gelu_po_kernel(
             raw = w_raw[n, h][:] if n == 1 else w2_raw[:, :, h * HALF : (h + 1) * HALF]
             src = raw.rearrange("p j (m t) -> p m j t", t=PACK)
             if (n, h) == (1, 1):
-                nc.vector.tensor_copy(dst, src)
+                nc.vector.tensor_copy(dst[:, :44], src[:, :44])
+                nc.scalar.copy(dst[:, 44:], src[:, 44:])
             else:
                 nc.scalar.copy(dst, src)
 
         def quant_w(n):
-            nc.vector.quantize_mx(out=w_c[n][:].bitcast(FP8X4), scales=w_s[n][:], in_=w_bf[n][:])
+            parts = 1 if n == 2 else 2
+            wid = H // parts
+            for i in range(parts):
+                cols = slice(i * wid, (i + 1) * wid)
+                nc.vector.quantize_mx(
+                    out=w_c[n][:, cols].bitcast(FP8X4), scales=w_s[n][:, cols], in_=w_bf[n][:, i * wid * PACK : (i + 1) * wid * PACK]
+                )
 
         z_c = {n: keep.tile([P, S], U32, name="z_c%d" % n, align_bytes=64) for n in (1, 2)}
         z_s = {n: keep.tile([P, S], U8, name="z_s%d" % n, align_bytes=64) for n in (1, 2)}
@@ -136,8 +155,10 @@ def tile_picked_expertpair_gelu_po_kernel(
         nz = {}
 
         def negate(c):
-            nz[c] = keep.tile([P, CH * PACK], BF16, name="nz%d" % c, align_bytes=64)
-            nc.vector.tensor_scalar_mul(nz[c][:], z_bf[2, c], -1.0)
+            if c == 0:
+                z_all["neg"] = keep.tile([P, S * PACK], BF16, name="nz", tag="w_bf1", align_bytes=64)
+            nz[c] = z_all["neg"][:, c * CH * PACK : (c + 1) * CH * PACK]
+            nc.vector.tensor_scalar_mul(nz[c], z_bf[2, c], -1.0)
 
         ww = keep.tile([P, 2, N], U32, name="ww", align_bytes=64)
         dealt = {}
@@ -147,7 +168,7 @@ def tile_picked_expertpair_gelu_po_kernel(
                 ww[:].rearrange("p w (t m) -> p w m t", t=PACK),
                 ww_raw[:].bitcast(U32).rearrange("p w (m t) -> p w m t", t=PACK),
             )
-            ws = keep.tile([P, N], U8, name="ws", tag="ww_raw", align_bytes=64)
+            ws = keep.tile([P, N], U8, name="ws", align_bytes=64)
             nc.vector.tensor_copy(ws[:].rearrange("p (t m) -> p t m", t=PACK), ws_raw[:].rearrange("p (m t) -> p t m", t=PACK))
             dealt["ws"] = ws
 
@@ -225,18 +246,17 @@ def tile_picked_expertpair_gelu_po_kernel(
         cast_w(1, 0)
         cast_w(1, 1)
         quant_w(1)
-        for n, c in ((2, 0), (2, 1), (1, 0), (1, 1), (2, 2), (1, 2), (2, 3), (1, 3)):
+        for n, c in ((2, 0), (2, 1), (2, 2), (2, 3), (1, 0), (1, 1), (1, 2), (1, 3)):
             layer1(n, c)
         deal()
 
-        def hidden(c):
-            negate(c)
-            quant_z(2, c, nz[c][:])
-            quant_z(1, c, z_bf[1, c])
-
-        hidden(0)
-        hidden(1)
         gather_q(3)
+        for c in range(NCH):
+            negate(c)
+        for c in range(NCH):
+            quant_z(2, c, nz[c])
+        quant_z(1, 0, z_bf[1, 0])
+        quant_z(1, 1, z_bf[1, 1])
         for c in range(NCH + 2):
             if c == 0:
                 layer2_d(0)
@@ -245,7 +265,7 @@ def tile_picked_expertpair_gelu_po_kernel(
                 layer2_d(c + 1)
                 layer2_b(c + 1)
             if c + 2 < NCH:
-                hidden(c + 2)
+                quant_z(1, c + 2, z_bf[1, c + 2])
             if c < NCH:
                 mul(c)
             if c >= 2:

@@ -63,7 +63,7 @@ def tile_picked_expertpair_gelu_po_kernel(
         def load_ws(eng, i, q):
             sc = (w3_scales, w4_scales)[i]
             eng.dma_start(
-                ws_raw[32 * q + 4 * i : 32 * q + 4 * i + 4, :].bitcast(I32), sc[0, 4 * q : 4 * q + 4, :].bitcast(I32)
+                ws_raw[32 * q + 4 * i + 4 : 32 * q + 4 * i + 8, :].bitcast(I32), sc[0, 4 * q : 4 * q + 4, :].bitcast(I32)
             )
 
         load_mix(0)
@@ -80,12 +80,12 @@ def tile_picked_expertpair_gelu_po_kernel(
         load_mix(2)
         load_ws(nc.sync, 0, 0)
         load_ws(nc.sync, 0, 1)
-        nc.sync.dma_start(xw[:], x_words[0].rearrange("p n t -> p (n t)").bitcast(I32))
+        load_w(1, 0)
         load_ws(nc.sync, 0, 2)
         load_ws(nc.sync, 0, 3)
-        load_w(1, 0)
-        load_mix(3)
+        nc.sync.dma_start(xw[:], x_words[0].rearrange("p n t -> p (n t)").bitcast(I32))
         load_w(1, 1)
+        load_mix(3)
         nc.sync.dma_start(ww_raw[:, 1, :], w4_words[0].rearrange("p n t -> p (n t)").bitcast(I32))
         nc.sync.dma_start(ww_raw[:, 0, :], w3_words[0].rearrange("p n t -> p (n t)").bitcast(I32))
 
@@ -108,8 +108,7 @@ def tile_picked_expertpair_gelu_po_kernel(
             raw = w_raw[n, h][:] if n == 1 else w2_raw[:, :, h * HALF : (h + 1) * HALF]
             src = raw.rearrange("p j (m t) -> p m j t", t=PACK)
             if (n, h) == (1, 1):
-                nc.vector.tensor_copy(dst[:, :44], src[:, :44])
-                nc.scalar.copy(dst[:, 44:], src[:, 44:])
+                nc.vector.tensor_copy(dst.rearrange("p m j t -> p m t j"), src.rearrange("p m j t -> p m t j"))
             else:
                 nc.scalar.copy(dst, src)
 
@@ -129,7 +128,7 @@ def tile_picked_expertpair_gelu_po_kernel(
 
         def layer1(n, c):
             cols = slice(c * CH, (c + 1) * CH)
-            bank = psum.tile([P, PACK, CH], F32, name="hid", tag="bank", bufs=8)
+            bank = psum.tile([P, PACK, CH], F32, name="hid%d%d" % (n, c), tag="bank%d%d" % (n, c))
             for t in range(PACK):
                 tc_ = slice(t * P, (t + 1) * P)
                 nc.tensor.matmul_mx(
@@ -142,7 +141,7 @@ def tile_picked_expertpair_gelu_po_kernel(
                     stop=True,
                 )
             if c == 0:
-                z_all[n] = keep.tile([P, S * PACK], BF16, name="z_bf%d" % n, tag="w_raw10" if n == 2 else "z_bf1", align_bytes=64)
+                z_all[n] = keep.tile([P, S * PACK], BF16, name="z_bf%d" % n, align_bytes=64)
             z_bf[n, c] = z_all[n][:, c * CH * PACK : (c + 1) * CH * PACK]
             nc.scalar.activation(
                 z_bf[n, c].rearrange("p (s t) -> p s t", t=PACK), bank[:].rearrange("p t s -> p s t"), ACT.Gelu_apprx_tanh
@@ -165,8 +164,8 @@ def tile_picked_expertpair_gelu_po_kernel(
 
         def deal():
             nc.vector.tensor_copy(
-                ww[:].rearrange("p w (t m) -> p w m t", t=PACK),
-                ww_raw[:].bitcast(U32).rearrange("p w (m t) -> p w m t", t=PACK),
+                ww[:].rearrange("p w (t g i) -> p w g t i", t=PACK, i=4),
+                ww_raw[:].bitcast(U32).rearrange("p w (g i t) -> p w g t i", t=PACK, i=4),
             )
             ws = keep.tile([P, N], U8, name="ws", align_bytes=64)
             nc.vector.tensor_copy(ws[:].rearrange("p (t m) -> p t m", t=PACK), ws_raw[:].rearrange("p (m t) -> p t m", t=PACK))
@@ -179,7 +178,7 @@ def tile_picked_expertpair_gelu_po_kernel(
             nc.tensor.matmul_mx(
                 out=bank[:, t, :],
                 lhsT=ww[:, i, tc_].bitcast(FP8X4),
-                lhsT_scale=dealt["ws"][4 * i : P, tc_],
+                lhsT_scale=dealt["ws"][4 * i + 4 : P, tc_],
                 rhs=z_c[n][:, cols].bitcast(FP8X4),
                 rhs_scale=z_s[n][:, cols],
                 start=start,
@@ -189,14 +188,14 @@ def tile_picked_expertpair_gelu_po_kernel(
         nb = {}
 
         def layer2_b(c):
-            nb[c] = psum.tile([P, PACK, CH], F32, name="nb%d" % c, tag="bank", bufs=8)
+            nb[c] = psum.tile([P, PACK, CH], F32, name="nb%d" % c, tag="bank1%d" % c)
             for t in range(PACK):
                 pass2(nb[c], t, c, 2, True, True)
 
         diff = {}
 
         def layer2_d(c):
-            diff[c] = psum.tile([P, PACK, CH], F32, name="diff", tag="bank", bufs=8)
+            diff[c] = psum.tile([P, PACK, CH], F32, name="diff%d" % c, tag="bank2%d" % c)
             for t in range(PACK):
                 pass2(diff[c], t, c, 1, True, False)
                 pass2(diff[c], t, c, 2, False, True)
@@ -251,21 +250,16 @@ def tile_picked_expertpair_gelu_po_kernel(
         deal()
 
         gather_q(3)
-        for c in range(NCH):
-            negate(c)
-        for c in range(NCH):
-            quant_z(2, c, nz[c])
-        quant_z(1, 0, z_bf[1, 0])
-        quant_z(1, 1, z_bf[1, 1])
+        for c0 in (0, 2):
+            for c in (c0, c0 + 1):
+                negate(c)
+            for c in (c0, c0 + 1):
+                quant_z(2, c, nz[c])
+            for c in (c0, c0 + 1):
+                quant_z(1, c, z_bf[1, c])
+                layer2_d(c)
+                layer2_b(c)
         for c in range(NCH + 2):
-            if c == 0:
-                layer2_d(0)
-                layer2_b(0)
-            if c + 1 < NCH:
-                layer2_d(c + 1)
-                layer2_b(c + 1)
-            if c + 2 < NCH:
-                quant_z(1, c + 2, z_bf[1, c + 2])
             if c < NCH:
                 mul(c)
             if c >= 2:

@@ -28,7 +28,6 @@ def tile_picked_expertpair_gelu_po_kernel(
     nc = tc.nc
     with ExitStack() as ctx:
         keep = ctx.enter_context(tc.tile_pool(name="keep", bufs=1))
-        ring = ctx.enter_context(tc.tile_pool(name="ring", bufs=2))
         psum = ctx.enter_context(tc.psum_pool(name="psum", bufs=1))
 
         offs_t = keep.tile([P, S // 16], U16, name="offs_t")
@@ -36,58 +35,49 @@ def tile_picked_expertpair_gelu_po_kernel(
         xw = keep.tile([P, T], I32, name="xw", align_bytes=64)
         xs = keep.tile([P, T], U8, name="xs", align_bytes=64)
         ws_raw = keep.tile([P, N], U8, name="ws_raw", align_bytes=64)
-        ww_raw = keep.tile([P, 2, N], I32, name="ww_raw", tag="ww_raw", align_bytes=64)
+        ww_raw = {n: keep.tile([P, N], I32, name="ww_raw%d" % n, align_bytes=64) for n in (1, 2)}
         mix_t = [keep.tile([P, U], F32, name="mix%d" % t, align_bytes=64) for t in range(PACK)]
-        w_raw = {(1, h): keep.tile([P, PACK, HALF], F32, name="w_raw1%d" % h, tag="w_raw1%d" % h, align_bytes=64) for h in range(2)}
-        w2_raw = keep.tile([P, PACK, H], F32, name="w2_raw", align_bytes=64)
+        w_raw = {n: keep.tile([P, PACK, H], F32, name="w_raw%d" % n, align_bytes=64) for n in (1, 2)}
         warm = keep.tile([P, 1], F32, name="warm")
         warm2 = keep.tile([P, 1], F32, name="warm2")
 
-        nc.gpsimd.memset(ws_raw[:].bitcast(I32), 0)
         nc.vector.memset(xs[:].bitcast(I32), 0)
         nc.vector.memset(warm[:], 0.0)
+        nc.vector.memset(ws_raw[:].bitcast(I32), 0)
 
-        nc.sync.dma_start(task_t[:], task)
         mix_rows = mix.rearrange("(p t) u -> p t u", t=PACK)
         w_rows = {1: w1.rearrange("(p j) c -> p j c", j=PACK), 2: w2.rearrange("(p j) c -> p j c", j=PACK)}
+        words2 = {1: w3_words, 2: w4_words}
+        scales2 = {1: w3_scales, 2: w4_scales}
 
         def load_mix(t):
             nc.sync.dma_start(mix_t[t][:], mix_rows[:, t, :])
 
-        def load_w(n, h):
-            nc.sync.dma_start(w_raw[n, h][:], w_rows[n][:, :, h * HALF : (h + 1) * HALF])
+        def load_ws(eng, n):
+            for q in range(4):
+                eng.dma_start(
+                    ws_raw[32 * q + 4 * n : 32 * q + 4 * n + 4, :].bitcast(I32), scales2[n][0, 4 * q : 4 * q + 4, :].bitcast(I32)
+                )
 
-        def load_xs(q):
-            nc.sync.dma_start(xs[32 * q : 32 * q + 4, :].bitcast(I32), x_scales[0, 4 * q : 4 * q + 4, :].bitcast(I32))
+        def load_ww(n):
+            nc.sync.dma_start(ww_raw[n][:], words2[n][0].rearrange("p n t -> p (n t)").bitcast(I32))
 
-        def load_ws(eng, i, q):
-            sc = (w3_scales, w4_scales)[i]
-            eng.dma_start(
-                ws_raw[32 * q + 4 * i + 4 : 32 * q + 4 * i + 8, :].bitcast(I32), sc[0, 4 * q : 4 * q + 4, :].bitcast(I32)
-            )
-
-        load_mix(0)
         nc.scalar.activation(warm2[:], warm[:], ACT.Gelu_apprx_tanh)
-        for q in range(4):
-            load_ws(nc.gpsimd, 1, q)
+        nc.sync.dma_start(task_t[:], task)
+        load_mix(0)
         load_mix(1)
         nc.sync.dma_start(offs_t[:], offs)
-        load_xs(0)
-        load_xs(1)
-        nc.sync.dma_start(w2_raw[:], w_rows[2])
-        load_xs(2)
-        load_xs(3)
+        for q in range(4):
+            nc.sync.dma_start(xs[32 * q : 32 * q + 4, :].bitcast(I32), x_scales[0, 4 * q : 4 * q + 4, :].bitcast(I32))
+        nc.sync.dma_start(w_raw[2][:], w_rows[2])
         load_mix(2)
-        load_ws(nc.sync, 0, 0)
-        load_ws(nc.sync, 0, 1)
-        load_w(1, 0)
-        load_ws(nc.sync, 0, 2)
-        load_ws(nc.sync, 0, 3)
+        load_ws(nc.sync, 2)
+        nc.sync.dma_start(w_raw[1][:], w_rows[1])
+        load_ws(nc.sync, 1)
         nc.sync.dma_start(xw[:], x_words[0].rearrange("p n t -> p (n t)").bitcast(I32))
-        load_w(1, 1)
         load_mix(3)
-        nc.sync.dma_start(ww_raw[:, 1, :], w4_words[0].rearrange("p n t -> p (n t)").bitcast(I32))
-        nc.sync.dma_start(ww_raw[:, 0, :], w3_words[0].rearrange("p n t -> p (n t)").bitcast(I32))
+        load_ww(2)
+        load_ww(1)
 
         q4 = keep.tile([P, PACK, S], F32, name="q4", align_bytes=64)
 
@@ -97,37 +87,43 @@ def tile_picked_expertpair_gelu_po_kernel(
                     q4[:, t, h * HALF : (h + 1) * HALF], mix_t[t][:].indirect(task_t[:, h * 16 : (h + 1) * 16])
                 )
 
-        xg_w = keep.tile([P, S], U32, name="xg_w", align_bytes=64)
+        xg_w = [keep.tile([P, HALF], U32, name="xg_w%d" % h, align_bytes=64) for h in range(2)]
         xg_s = keep.tile([P, S], U8, name="xg_s", align_bytes=64)
-        w_bf = {n: keep.tile([P, PACK * H], BF16, name="w_bf%d" % n, tag="w_bf%d" % n, align_bytes=64) for n in (1, 2)}
+        w_bf = {(n, h): keep.tile([P, 2 * H], BF16, name="w_bf%d%d" % (n, h), align_bytes=64) for n in (1, 2) for h in range(2)}
         w_c = {n: keep.tile([P, H], U32, name="w_c%d" % n, align_bytes=64) for n in (1, 2)}
         w_s = {n: keep.tile([P, H], U8, name="w_s%d" % n, align_bytes=64) for n in (1, 2)}
 
-        def cast_w(n, h):
-            dst = w_bf[n][:].rearrange("p (t m j) -> p m j t", t=PACK, j=PACK)[:, h * 64 : (h + 1) * 64]
-            raw = w_raw[n, h][:] if n == 1 else w2_raw[:, :, h * HALF : (h + 1) * HALF]
-            src = raw.rearrange("p j (m t) -> p m j t", t=PACK)
-            if (n, h) == (1, 1):
+        def cast_w(n, h, on_vector):
+            dst = w_bf[n, h][:].rearrange("p (t m j) -> p m j t", t=2, j=PACK)
+            src = w_raw[n][:].rearrange("p j (m t) -> p m j t", t=PACK)[:, :, :, 2 * h : 2 * h + 2]
+            if on_vector:
                 nc.vector.tensor_copy(dst.rearrange("p m j t -> p m t j"), src.rearrange("p m j t -> p m t j"))
             else:
                 nc.scalar.copy(dst, src)
 
-        def quant_w(n):
-            parts = 1 if n == 2 else 2
-            wid = H // parts
-            for i in range(parts):
-                cols = slice(i * wid, (i + 1) * wid)
-                nc.vector.quantize_mx(
-                    out=w_c[n][:, cols].bitcast(FP8X4), scales=w_s[n][:, cols], in_=w_bf[n][:, i * wid * PACK : (i + 1) * wid * PACK]
-                )
+        def quant_w(n, h):
+            cols = slice(h * HALF, (h + 1) * HALF)
+            nc.vector.quantize_mx(out=w_c[n][:, cols].bitcast(FP8X4), scales=w_s[n][:, cols], in_=w_bf[n, h][:])
 
-        z_c = {n: keep.tile([P, S], U32, name="z_c%d" % n, align_bytes=64) for n in (1, 2)}
-        z_s = {n: keep.tile([P, S], U8, name="z_s%d" % n, align_bytes=64) for n in (1, 2)}
+        ww = {n: keep.tile([P, N], U32, name="ww%d" % n, align_bytes=64) for n in (1, 2)}
+        ws = keep.tile([P, N], U8, name="ws", align_bytes=64)
+
+        def deal_words(n):
+            nc.vector.tensor_copy(
+                ww[n][:].rearrange("p (t g i) -> p g t i", t=PACK, i=4),
+                ww_raw[n][:].bitcast(U32).rearrange("p (g i t) -> p g t i", t=PACK, i=4),
+            )
+
+        def deal_scales():
+            nc.vector.tensor_copy(ws[:].rearrange("p (t m) -> p t m", t=PACK), ws_raw[:].rearrange("p (m t) -> p t m", t=PACK))
+
         z_bf = {}
-        z_all = {}
+        z_c = {}
+        z_s = {}
 
         def layer1(n, c):
             cols = slice(c * CH, (c + 1) * CH)
+            gcols = slice(c % 2 * CH, (c % 2 + 1) * CH)
             bank = psum.tile([P, PACK, CH], F32, name="hid%d%d" % (n, c), tag="bank%d%d" % (n, c))
             for t in range(PACK):
                 tc_ = slice(t * P, (t + 1) * P)
@@ -135,70 +131,53 @@ def tile_picked_expertpair_gelu_po_kernel(
                     out=bank[:, t, :],
                     lhsT=w_c[n][:, tc_].bitcast(FP8X4),
                     lhsT_scale=w_s[n][:, tc_],
-                    rhs=xg_w[:, cols].bitcast(FP8X4),
+                    rhs=xg_w[c // 2][:, gcols].bitcast(FP8X4),
                     rhs_scale=xg_s[:, cols],
                     start=True,
                     stop=True,
                 )
-            if c == 0:
-                z_all[n] = keep.tile([P, S * PACK], BF16, name="z_bf%d" % n, align_bytes=64)
-            z_bf[n, c] = z_all[n][:, c * CH * PACK : (c + 1) * CH * PACK]
+            z_bf[n, c] = keep.tile([P, CH * PACK], BF16, name="z_bf%d%d" % (n, c), align_bytes=64)
             nc.scalar.activation(
-                z_bf[n, c].rearrange("p (s t) -> p s t", t=PACK), bank[:].rearrange("p t s -> p s t"), ACT.Gelu_apprx_tanh
+                z_bf[n, c][:].rearrange("p (s t) -> p s t", t=PACK), bank[:].rearrange("p t s -> p s t"), ACT.Gelu_apprx_tanh
             )
-
-        def quant_z(n, c, src):
-            cols = slice(c * CH, (c + 1) * CH)
-            nc.vector.quantize_mx(out=z_c[n][:, cols].bitcast(FP8X4), scales=z_s[n][:, cols], in_=src)
 
         nz = {}
 
         def negate(c):
-            if c == 0:
-                z_all["neg"] = keep.tile([P, S * PACK], BF16, name="nz", tag="w_bf1", align_bytes=64)
-            nz[c] = z_all["neg"][:, c * CH * PACK : (c + 1) * CH * PACK]
-            nc.vector.tensor_scalar_mul(nz[c], z_bf[2, c], -1.0)
+            nz[c] = keep.tile([P, CH * PACK], BF16, name="nz%d" % c, align_bytes=64)
+            nc.vector.tensor_scalar_mul(nz[c][:], z_bf[2, c][:], -1.0)
 
-        ww = keep.tile([P, 2, N], U32, name="ww", align_bytes=64)
-        dealt = {}
+        def quant_z(n, c):
+            z_c[n, c] = keep.tile([P, CH], U32, name="z_c%d%d" % (n, c), align_bytes=64)
+            z_s[n, c] = keep.tile([P, CH], U8, name="z_s%d%d" % (n, c), align_bytes=64)
+            src = nz[c] if n == 2 else z_bf[1, c]
+            nc.vector.quantize_mx(out=z_c[n, c][:].bitcast(FP8X4), scales=z_s[n, c][:], in_=src[:])
 
-        def deal():
-            nc.vector.tensor_copy(
-                ww[:].rearrange("p w (t g i) -> p w g t i", t=PACK, i=4),
-                ww_raw[:].bitcast(U32).rearrange("p w (g i t) -> p w g t i", t=PACK, i=4),
-            )
-            ws = keep.tile([P, N], U8, name="ws", align_bytes=64)
-            nc.vector.tensor_copy(ws[:].rearrange("p (t m) -> p t m", t=PACK), ws_raw[:].rearrange("p (m t) -> p t m", t=PACK))
-            dealt["ws"] = ws
-
-        def pass2(bank, t, c, n, start, stop):
-            cols = slice(c * CH, (c + 1) * CH)
-            tc_ = slice(t * P, (t + 1) * P)
-            i = n - 1
-            nc.tensor.matmul_mx(
-                out=bank[:, t, :],
-                lhsT=ww[:, i, tc_].bitcast(FP8X4),
-                lhsT_scale=dealt["ws"][4 * i + 4 : P, tc_],
-                rhs=z_c[n][:, cols].bitcast(FP8X4),
-                rhs_scale=z_s[n][:, cols],
-                start=start,
-                stop=stop,
-            )
+        def passes2(bank, n, c, opens, closes, lone):
+            for t in range(PACK):
+                tc_ = slice(t * P, (t + 1) * P)
+                nc.tensor.matmul_mx(
+                    out=bank[:, t, :],
+                    lhsT=ww[n][:, tc_].bitcast(FP8X4),
+                    lhsT_scale=ws[4 * n : P, tc_],
+                    rhs=z_c[n, c][:].bitcast(FP8X4),
+                    rhs_scale=z_s[n, c][:],
+                    start=lone or (opens and t == 0),
+                    stop=lone or (closes and t == PACK - 1),
+                )
 
         nb = {}
-
-        def layer2_b(c):
-            nb[c] = psum.tile([P, PACK, CH], F32, name="nb%d" % c, tag="bank1%d" % c)
-            for t in range(PACK):
-                pass2(nb[c], t, c, 2, True, True)
-
         diff = {}
 
-        def layer2_d(c):
+        def hidden(c):
+            negate(c)
+            quant_z(2, c)
             diff[c] = psum.tile([P, PACK, CH], F32, name="diff%d" % c, tag="bank2%d" % c)
-            for t in range(PACK):
-                pass2(diff[c], t, c, 1, True, False)
-                pass2(diff[c], t, c, 2, False, True)
+            passes2(diff[c], 2, c, True, False, False)
+            quant_z(1, c)
+            passes2(diff[c], 1, c, False, True, False)
+            nb[c] = psum.tile([P, PACK, CH], F32, name="nb%d" % c, tag="bank1%d" % c)
+            passes2(nb[c], 2, c, False, False, True)
 
         o_c = keep.tile([P, S], I32, name="o_c", align_bytes=64)
         o_s = keep.tile([P, S], U8, name="o_s", align_bytes=64)
@@ -210,7 +189,7 @@ def tile_picked_expertpair_gelu_po_kernel(
 
         def mul(c):
             cols = slice(c * CH, (c + 1) * CH)
-            prod[c] = ring.tile([P, PACK, CH], F32, name="prod", tag="prod")
+            prod[c] = keep.tile([P, PACK, CH], F32, name="prod%d" % c, align_bytes=64)
             nc.vector.tensor_tensor(prod[c][:], diff[c][:], q4[:, :, cols], ALU.mult)
 
         def sub(c):
@@ -230,45 +209,42 @@ def tile_picked_expertpair_gelu_po_kernel(
         def quant_y(c):
             cols = slice(c * CH, (c + 1) * CH)
             nc.vector.quantize_mx(out=o_c[:, cols].bitcast(FP8X4), scales=o_s[:, cols], in_=y_bf[c][:])
+            nc.sync.dma_start(o1[:, cols], o_c[:, cols])
 
         gather_q(0)
         gather_q(1)
-        gather_q(2)
+        cast_w(2, 0, False)
+        cast_w(2, 1, False)
         nc.vector.tensor_copy(xg_s[:], xs[:].indirect(offs_t[:]))
+        quant_w(2, 0)
+        quant_w(2, 1)
+        gather_q(2)
+        cast_w(1, 0, False)
+        cast_w(1, 1, True)
+        quant_w(1, 1)
+        quant_w(1, 0)
         for h in range(2):
-            nc.vector.tensor_copy(
-                xg_w[:, h * HALF : (h + 1) * HALF], xw[:].bitcast(U32).indirect(offs_t[:, h * 16 : (h + 1) * 16])
-            )
-        cast_w(2, 0)
-        cast_w(2, 1)
-        quant_w(2)
-        cast_w(1, 0)
-        cast_w(1, 1)
-        quant_w(1)
-        for n, c in ((2, 0), (2, 1), (2, 2), (2, 3), (1, 0), (1, 1), (1, 2), (1, 3)):
-            layer1(n, c)
-        deal()
-
+            nc.vector.tensor_copy(xg_w[h][:], xw[:].bitcast(U32).indirect(offs_t[:, h * 16 : (h + 1) * 16]))
+        deal_scales()
         gather_q(3)
-        for c0 in (0, 2):
-            for c in (c0, c0 + 1):
-                negate(c)
-            for c in (c0, c0 + 1):
-                quant_z(2, c, nz[c])
-            for c in (c0, c0 + 1):
-                quant_z(1, c, z_bf[1, c])
-                layer2_d(c)
-                layer2_b(c)
-        for c in range(NCH + 2):
-            if c < NCH:
-                mul(c)
-            if c >= 2:
+        deal_words(2)
+        deal_words(1)
+        for c in range(NCH - 1):
+            layer1(2, c)
+            layer1(1, c)
+        hidden(0)
+        layer1(2, NCH - 1)
+        layer1(1, NCH - 1)
+        hidden(1)
+        for c in range(NCH):
+            mul(c)
+            if c + 2 < NCH:
+                hidden(c + 2)
+            else:
                 quant_y(c - 2)
-            if c < NCH:
-                sub(c)
-        last = S - CH
-        nc.sync.dma_start(o1[:, :last], o_c[:, :last])
-        nc.sync.dma_start(o1[:, last:], o_c[:, last:])
+            sub(c)
+        quant_y(NCH - 2)
+        quant_y(NCH - 1)
         for q in range(4):
             eng = nc.scalar if q % 2 else nc.sync
             eng.dma_start(out_2[0, 4 * q : 4 * q + 4, :].bitcast(I32), o_s[32 * q : 32 * q + 4, :].bitcast(I32))

@@ -20,6 +20,7 @@ PACK = 4
 CH = 128
 NCH = S // CH
 HALF = 256
+POOL_CHUNK = 1
 
 
 def tile_picked_expertpair_gelu_po_kernel(
@@ -37,13 +38,14 @@ def tile_picked_expertpair_gelu_po_kernel(
         ws_raw = keep.tile([P, N], U8, name="ws_raw", align_bytes=64)
         ww_raw = {n: keep.tile([P, N], I32, name="ww_raw%d" % n, align_bytes=64) for n in (1, 2)}
         mix_t = [keep.tile([P, U], F32, name="mix%d" % t, align_bytes=64) for t in range(PACK)]
-        w_raw = {n: keep.tile([P, PACK, H], F32, name="w_raw%d" % n, align_bytes=64) for n in (1, 2)}
+        w2_raw = keep.tile([P, PACK, H], F32, name="w2_raw", align_bytes=64)
+        w1_raw = [keep.tile([P, PACK, HALF], F32, name="w1_raw%d" % h, align_bytes=64) for h in range(2)]
         warm = keep.tile([P, 1], F32, name="warm")
         warm2 = keep.tile([P, 1], F32, name="warm2")
 
         nc.vector.memset(xs[:].bitcast(I32), 0)
         nc.vector.memset(warm[:], 0.0)
-        nc.vector.memset(ws_raw[:].bitcast(I32), 0)
+        nc.gpsimd.memset(ws_raw[:].bitcast(I32), 0)
 
         mix_rows = mix.rearrange("(p t) u -> p t u", t=PACK)
         w_rows = {1: w1.rearrange("(p j) c -> p j c", j=PACK), 2: w2.rearrange("(p j) c -> p j c", j=PACK)}
@@ -64,17 +66,18 @@ def tile_picked_expertpair_gelu_po_kernel(
 
         nc.scalar.activation(warm2[:], warm[:], ACT.Gelu_apprx_tanh)
         nc.sync.dma_start(task_t[:], task)
+        load_ws(nc.gpsimd, 2)
         load_mix(0)
         load_mix(1)
         nc.sync.dma_start(offs_t[:], offs)
         for q in range(4):
             nc.sync.dma_start(xs[32 * q : 32 * q + 4, :].bitcast(I32), x_scales[0, 4 * q : 4 * q + 4, :].bitcast(I32))
-        nc.sync.dma_start(w_raw[2][:], w_rows[2])
+        nc.sync.dma_start(w2_raw[:], w_rows[2])
         load_mix(2)
-        load_ws(nc.sync, 2)
-        nc.sync.dma_start(w_raw[1][:], w_rows[1])
         load_ws(nc.sync, 1)
+        nc.sync.dma_start(w1_raw[0][:], w_rows[1][:, :, :HALF])
         nc.sync.dma_start(xw[:], x_words[0].rearrange("p n t -> p (n t)").bitcast(I32))
+        nc.sync.dma_start(w1_raw[1][:], w_rows[1][:, :, HALF:])
         load_mix(3)
         load_ww(2)
         load_ww(1)
@@ -89,21 +92,32 @@ def tile_picked_expertpair_gelu_po_kernel(
 
         xg_w = [keep.tile([P, HALF], U32, name="xg_w%d" % h, align_bytes=64) for h in range(2)]
         xg_s = keep.tile([P, S], U8, name="xg_s", align_bytes=64)
-        w_bf = {(n, h): keep.tile([P, 2 * H], BF16, name="w_bf%d%d" % (n, h), align_bytes=64) for n in (1, 2) for h in range(2)}
+        w_bf = {(n, h): keep.tile([P, 2 * H], BF16, name="w_bf%d%d" % (n, h), tag="w_bf%d%d" % (n, h), align_bytes=64) for n in (1, 2) for h in range(2)}
         w_c = {n: keep.tile([P, H], U32, name="w_c%d" % n, align_bytes=64) for n in (1, 2)}
         w_s = {n: keep.tile([P, H], U8, name="w_s%d" % n, align_bytes=64) for n in (1, 2)}
 
-        def cast_w(n, h, on_vector):
-            dst = w_bf[n, h][:].rearrange("p (t m j) -> p m j t", t=2, j=PACK)
-            src = w_raw[n][:].rearrange("p j (m t) -> p m j t", t=PACK)[:, :, :, 2 * h : 2 * h + 2]
-            if on_vector:
+        def cast_w2(h):
+            dst = w_bf[2, h][:].rearrange("p (t m j) -> p m j t", t=2, j=PACK)
+            nc.scalar.copy(dst, w2_raw[:].rearrange("p j (m t) -> p m j t", t=PACK)[:, :, :, 2 * h : 2 * h + 2])
+
+        def quant_w2(h):
+            cols = slice(h * HALF, (h + 1) * HALF)
+            nc.vector.quantize_mx(out=w_c[2][:, cols].bitcast(FP8X4), scales=w_s[2][:, cols], in_=w_bf[2, h][:])
+
+        def cast_w1(h):
+            dst = w_bf[1, h][:].rearrange("p (t m j) -> p m j t", t=PACK, j=PACK)
+            src = w1_raw[h][:].rearrange("p j (m t) -> p m j t", t=PACK)
+            if h:
                 nc.vector.tensor_copy(dst.rearrange("p m j t -> p m t j"), src.rearrange("p m j t -> p m t j"))
             else:
                 nc.scalar.copy(dst, src)
 
-        def quant_w(n, h):
-            cols = slice(h * HALF, (h + 1) * HALF)
-            nc.vector.quantize_mx(out=w_c[n][:, cols].bitcast(FP8X4), scales=w_s[n][:, cols], in_=w_bf[n, h][:])
+        def quant_w1(h):
+            for t in range(PACK):
+                cols = slice(t * P + h * 64, t * P + (h + 1) * 64)
+                nc.vector.quantize_mx(
+                    out=w_c[1][:, cols].bitcast(FP8X4), scales=w_s[1][:, cols], in_=w_bf[1, h][:, t * HALF : (t + 1) * HALF]
+                )
 
         ww = {n: keep.tile([P, N], U32, name="ww%d" % n, align_bytes=64) for n in (1, 2)}
         ws = keep.tile([P, N], U8, name="ws", align_bytes=64)
@@ -144,7 +158,7 @@ def tile_picked_expertpair_gelu_po_kernel(
         nz = {}
 
         def negate(c):
-            nz[c] = keep.tile([P, CH * PACK], BF16, name="nz%d" % c, align_bytes=64)
+            nz[c] = keep.tile([P, CH * PACK], BF16, name="nz%d" % c, tag="w_bf11" if c == 0 else "nz%d" % c, align_bytes=64)
             nc.vector.tensor_scalar_mul(nz[c][:], z_bf[2, c][:], -1.0)
 
         def quant_z(n, c):
@@ -168,6 +182,7 @@ def tile_picked_expertpair_gelu_po_kernel(
 
         nb = {}
         diff = {}
+        nb_sb = {}
 
         def hidden(c):
             negate(c)
@@ -178,6 +193,9 @@ def tile_picked_expertpair_gelu_po_kernel(
             passes2(diff[c], 1, c, False, True, False)
             nb[c] = psum.tile([P, PACK, CH], F32, name="nb%d" % c, tag="bank1%d" % c)
             passes2(nb[c], 2, c, False, False, True)
+            if c == POOL_CHUNK:
+                nb_sb[c] = keep.tile([P, PACK, CH], F32, name="nb_sb%d" % c, align_bytes=64)
+                nc.scalar.copy(nb_sb[c][:], nb[c][:])
 
         o_c = keep.tile([P, S], I32, name="o_c", align_bytes=64)
         o_s = keep.tile([P, S], U8, name="o_s", align_bytes=64)
@@ -195,7 +213,10 @@ def tile_picked_expertpair_gelu_po_kernel(
         def sub(c):
             cols = slice(c * CH, (c + 1) * CH)
             y[c] = keep.tile([P, PACK, CH], F32, name="y%d" % c, align_bytes=64)
-            nc.vector.tensor_tensor(y[c][:], prod[c][:], nb[c][:], ALU.subtract)
+            if c == POOL_CHUNK:
+                nc.gpsimd.tensor_tensor(y[c][:], prod[c][:], nb_sb[c][:], ALU.subtract)
+            else:
+                nc.vector.tensor_tensor(y[c][:], prod[c][:], nb[c][:], ALU.subtract)
             nc.sync.dma_start(out_rows[:, :, cols], y[c][:])
             y_bf[c] = keep.tile([P, CH * PACK], BF16, name="y_bf%d" % c, align_bytes=64)
             dst = y_bf[c][:].rearrange("p (g i t) -> p g t i", i=4, t=PACK)
@@ -209,42 +230,44 @@ def tile_picked_expertpair_gelu_po_kernel(
         def quant_y(c):
             cols = slice(c * CH, (c + 1) * CH)
             nc.vector.quantize_mx(out=o_c[:, cols].bitcast(FP8X4), scales=o_s[:, cols], in_=y_bf[c][:])
-            nc.sync.dma_start(o1[:, cols], o_c[:, cols])
+            if c % 2:
+                first = 0 if c == 1 else c * CH
+                last = S - CH if c == 1 else S
+                nc.sync.dma_start(o1[:, first:last], o_c[:, first:last])
 
         gather_q(0)
         gather_q(1)
-        cast_w(2, 0, False)
-        cast_w(2, 1, False)
         nc.vector.tensor_copy(xg_s[:], xs[:].indirect(offs_t[:]))
-        quant_w(2, 0)
-        quant_w(2, 1)
+        cast_w2(0)
+        cast_w2(1)
         gather_q(2)
-        cast_w(1, 0, False)
-        cast_w(1, 1, True)
-        quant_w(1, 1)
-        quant_w(1, 0)
+        quant_w2(0)
+        quant_w2(1)
+        cast_w1(0)
+        quant_w1(0)
+        deal_scales()
         for h in range(2):
             nc.vector.tensor_copy(xg_w[h][:], xw[:].bitcast(U32).indirect(offs_t[:, h * 16 : (h + 1) * 16]))
-        deal_scales()
+        cast_w1(1)
+        quant_w1(1)
         gather_q(3)
+        layer1(2, 0)
+        layer1(2, 1)
+        for c in range(NCH):
+            layer1(1, c)
+            if c + 2 < NCH:
+                layer1(2, c + 2)
         deal_words(2)
         deal_words(1)
-        for c in range(NCH - 1):
-            layer1(2, c)
-            layer1(1, c)
-        hidden(0)
-        layer1(2, NCH - 1)
-        layer1(1, NCH - 1)
-        hidden(1)
+        for c in range(NCH):
+            hidden(c)
         for c in range(NCH):
             mul(c)
-            if c + 2 < NCH:
-                hidden(c + 2)
-            else:
-                quant_y(c - 2)
+            if c == NCH - 1:
+                quant_y(0)
             sub(c)
-        quant_y(NCH - 2)
-        quant_y(NCH - 1)
+        for c in (2, 1, 3):
+            quant_y(c)
         for q in range(4):
             eng = nc.scalar if q % 2 else nc.sync
             eng.dma_start(out_2[0, 4 * q : 4 * q + 4, :].bitcast(I32), o_s[32 * q : 32 * q + 4, :].bitcast(I32))

@@ -40,11 +40,8 @@ def tile_picked_expertpair_gelu_po_kernel(
         mix_t = [keep.tile([P, U], F32, name="mix%d" % t, align_bytes=64) for t in range(PACK)]
         w2_raw = keep.tile([P, PACK, H], F32, name="w2_raw", align_bytes=64)
         w1_raw = [keep.tile([P, PACK, HALF], F32, name="w1_raw%d" % h, align_bytes=64) for h in range(2)]
-        warm = keep.tile([P, 1], F32, name="warm")
-        warm2 = keep.tile([P, 1], F32, name="warm2")
 
         nc.vector.memset(xs[:].bitcast(I32), 0)
-        nc.vector.memset(warm[:], 0.0)
         nc.gpsimd.memset(ws_raw[:].bitcast(I32), 0)
 
         mix_rows = mix.rearrange("(p t) u -> p t u", t=PACK)
@@ -64,7 +61,6 @@ def tile_picked_expertpair_gelu_po_kernel(
         def load_ww(n):
             nc.sync.dma_start(ww_raw[n][:], words2[n][0].rearrange("p n t -> p (n t)").bitcast(I32))
 
-        nc.scalar.activation(warm2[:], warm[:], ACT.Gelu_apprx_tanh)
         nc.sync.dma_start(task_t[:], task)
         load_ws(nc.gpsimd, 2)
         load_mix(0)

@@ -20,7 +20,7 @@ PACK = 4
 CH = 128
 NCH = S // CH
 HALF = 256
-POOL_CHUNK = 1
+POOL_CHUNK = 0
 
 
 def tile_picked_expertpair_gelu_po_kernel(
@@ -39,10 +39,10 @@ def tile_picked_expertpair_gelu_po_kernel(
         ww_raw = {n: keep.tile([P, N], I32, name="ww_raw%d" % n, align_bytes=64) for n in (1, 2)}
         mix_t = [keep.tile([P, U], F32, name="mix%d" % t, align_bytes=64) for t in range(PACK)]
         w2_raw = keep.tile([P, PACK, H], F32, name="w2_raw", align_bytes=64)
-        w1_raw = [keep.tile([P, PACK, HALF], F32, name="w1_raw%d" % h, align_bytes=64) for h in range(2)]
+        w1_raw = [keep.tile([P, PACK, HALF], F32, name="w1_raw%d" % h, tag="w1_raw%d" % h, align_bytes=64) for h in range(2)]
 
         nc.vector.memset(xs[:].bitcast(I32), 0)
-        nc.gpsimd.memset(ws_raw[:].bitcast(I32), 0)
+        nc.vector.memset(ws_raw[:].bitcast(I32), 0)
 
         mix_rows = mix.rearrange("(p t) u -> p t u", t=PACK)
         w_rows = {1: w1.rearrange("(p j) c -> p j c", j=PACK), 2: w2.rearrange("(p j) c -> p j c", j=PACK)}
@@ -62,17 +62,17 @@ def tile_picked_expertpair_gelu_po_kernel(
             nc.sync.dma_start(ww_raw[n][:], words2[n][0].rearrange("p n t -> p (n t)").bitcast(I32))
 
         nc.sync.dma_start(task_t[:], task)
-        load_ws(nc.gpsimd, 2)
         load_mix(0)
-        load_mix(1)
         nc.sync.dma_start(offs_t[:], offs)
         for q in range(4):
             nc.sync.dma_start(xs[32 * q : 32 * q + 4, :].bitcast(I32), x_scales[0, 4 * q : 4 * q + 4, :].bitcast(I32))
         nc.sync.dma_start(w2_raw[:], w_rows[2])
+        load_mix(1)
+        load_ws(nc.sync, 2)
         load_mix(2)
-        load_ws(nc.sync, 1)
         nc.sync.dma_start(w1_raw[0][:], w_rows[1][:, :, :HALF])
         nc.sync.dma_start(xw[:], x_words[0].rearrange("p n t -> p (n t)").bitcast(I32))
+        load_ws(nc.sync, 1)
         nc.sync.dma_start(w1_raw[1][:], w_rows[1][:, :, HALF:])
         load_mix(3)
         load_ww(2)
@@ -80,8 +80,8 @@ def tile_picked_expertpair_gelu_po_kernel(
 
         q4 = keep.tile([P, PACK, S], F32, name="q4", align_bytes=64)
 
-        def gather_q(t):
-            for h in range(2):
+        def gather_q(t, halves=(0, 1)):
+            for h in halves:
                 nc.vector.tensor_copy(
                     q4[:, t, h * HALF : (h + 1) * HALF], mix_t[t][:].indirect(task_t[:, h * 16 : (h + 1) * 16])
                 )
@@ -116,7 +116,7 @@ def tile_picked_expertpair_gelu_po_kernel(
                 )
 
         ww = {n: keep.tile([P, N], U32, name="ww%d" % n, align_bytes=64) for n in (1, 2)}
-        ws = keep.tile([P, N], U8, name="ws", align_bytes=64)
+        dealt = {}
 
         def deal_words(n):
             nc.vector.tensor_copy(
@@ -125,6 +125,8 @@ def tile_picked_expertpair_gelu_po_kernel(
             )
 
         def deal_scales():
+            ws = keep.tile([P, N], U8, name="ws", tag="w1_raw1", align_bytes=64)
+            dealt["ws"] = ws
             nc.vector.tensor_copy(ws[:].rearrange("p (t m) -> p t m", t=PACK), ws_raw[:].rearrange("p (m t) -> p t m", t=PACK))
 
         z_bf = {}
@@ -146,22 +148,27 @@ def tile_picked_expertpair_gelu_po_kernel(
                     start=True,
                     stop=True,
                 )
-            z_bf[n, c] = keep.tile([P, CH * PACK], BF16, name="z_bf%d%d" % (n, c), align_bytes=64)
+            if (n, c) == (1, 0):
+                z_bf[n, c] = q4[:, PACK - 1, HALF:].bitcast(BF16)
+            else:
+                z_bf[n, c] = keep.tile([P, CH * PACK], BF16, name="z_bf%d%d" % (n, c), align_bytes=64)[:]
             nc.scalar.activation(
-                z_bf[n, c][:].rearrange("p (s t) -> p s t", t=PACK), bank[:].rearrange("p t s -> p s t"), ACT.Gelu_apprx_tanh
+                z_bf[n, c].rearrange("p (s t) -> p s t", t=PACK), bank[:].rearrange("p t s -> p s t"), ACT.Gelu_apprx_tanh
             )
 
         nz = {}
 
         def negate(c):
-            nz[c] = keep.tile([P, CH * PACK], BF16, name="nz%d" % c, tag="w_bf11" if c == 0 else "nz%d" % c, align_bytes=64)
-            nc.vector.tensor_scalar_mul(nz[c][:], z_bf[2, c][:], -1.0)
+            if c == 0:
+                nz["tile"] = keep.tile([P, S * PACK], BF16, name="nz", tag="w_bf11", align_bytes=64)
+            nz[c] = nz["tile"][:, c * CH * PACK : (c + 1) * CH * PACK]
+            nc.vector.tensor_scalar_mul(nz[c], z_bf[2, c], -1.0)
 
         def quant_z(n, c):
             z_c[n, c] = keep.tile([P, CH], U32, name="z_c%d%d" % (n, c), align_bytes=64)
             z_s[n, c] = keep.tile([P, CH], U8, name="z_s%d%d" % (n, c), align_bytes=64)
             src = nz[c] if n == 2 else z_bf[1, c]
-            nc.vector.quantize_mx(out=z_c[n, c][:].bitcast(FP8X4), scales=z_s[n, c][:], in_=src[:])
+            nc.vector.quantize_mx(out=z_c[n, c][:].bitcast(FP8X4), scales=z_s[n, c][:], in_=src)
 
         def passes2(bank, n, c, opens, closes, lone):
             for t in range(PACK):
@@ -169,7 +176,7 @@ def tile_picked_expertpair_gelu_po_kernel(
                 nc.tensor.matmul_mx(
                     out=bank[:, t, :],
                     lhsT=ww[n][:, tc_].bitcast(FP8X4),
-                    lhsT_scale=ws[4 * n : P, tc_],
+                    lhsT_scale=dealt["ws"][4 * n : P, tc_],
                     rhs=z_c[n, c][:].bitcast(FP8X4),
                     rhs_scale=z_s[n, c][:],
                     start=lone or (opens and t == 0),
@@ -187,6 +194,8 @@ def tile_picked_expertpair_gelu_po_kernel(
             passes2(diff[c], 2, c, True, False, False)
             quant_z(1, c)
             passes2(diff[c], 1, c, False, True, False)
+
+        def minus_b(c):
             nb[c] = psum.tile([P, PACK, CH], F32, name="nb%d" % c, tag="bank1%d" % c)
             passes2(nb[c], 2, c, False, False, True)
             if c == POOL_CHUNK:
@@ -199,7 +208,7 @@ def tile_picked_expertpair_gelu_po_kernel(
         o1 = out_1[0].rearrange("p n t -> p (n t)").bitcast(I32)
         prod = {}
         y = {}
-        y_bf = {}
+        y_bf = keep.tile([P, S * PACK], BF16, name="y_bf", align_bytes=64)
 
         def mul(c):
             cols = slice(c * CH, (c + 1) * CH)
@@ -214,8 +223,7 @@ def tile_picked_expertpair_gelu_po_kernel(
             else:
                 nc.vector.tensor_tensor(y[c][:], prod[c][:], nb[c][:], ALU.subtract)
             nc.sync.dma_start(out_rows[:, :, cols], y[c][:])
-            y_bf[c] = keep.tile([P, CH * PACK], BF16, name="y_bf%d" % c, align_bytes=64)
-            dst = y_bf[c][:].rearrange("p (g i t) -> p g t i", i=4, t=PACK)
+            dst = y_bf[:, c * CH * PACK : (c + 1) * CH * PACK].rearrange("p (g i t) -> p g t i", i=4, t=PACK)
             src = y[c][:].rearrange("p t (g i) -> p g t i", i=4)
             if c < NCH - 1:
                 nc.scalar.copy(dst, src)
@@ -223,17 +231,15 @@ def tile_picked_expertpair_gelu_po_kernel(
                 nc.scalar.copy(dst[:, :16], src[:, :16])
                 nc.vector.tensor_copy(dst[:, 16:], src[:, 16:])
 
-        def quant_y(c):
-            cols = slice(c * CH, (c + 1) * CH)
-            nc.vector.quantize_mx(out=o_c[:, cols].bitcast(FP8X4), scales=o_s[:, cols], in_=y_bf[c][:])
-            if c % 2:
-                first = 0 if c == 1 else c * CH
-                last = S - CH if c == 1 else S
-                nc.sync.dma_start(o1[:, first:last], o_c[:, first:last])
+        def quant_y(first, last):
+            cols = slice(first * CH, last * CH)
+            nc.vector.quantize_mx(
+                out=o_c[:, cols].bitcast(FP8X4), scales=o_s[:, cols], in_=y_bf[:, first * CH * PACK : last * CH * PACK]
+            )
 
         gather_q(0)
-        gather_q(1)
         nc.vector.tensor_copy(xg_s[:], xs[:].indirect(offs_t[:]))
+        gather_q(1)
         cast_w2(0)
         cast_w2(1)
         gather_q(2)
@@ -241,12 +247,12 @@ def tile_picked_expertpair_gelu_po_kernel(
         quant_w2(1)
         cast_w1(0)
         quant_w1(0)
-        deal_scales()
         for h in range(2):
             nc.vector.tensor_copy(xg_w[h][:], xw[:].bitcast(U32).indirect(offs_t[:, h * 16 : (h + 1) * 16]))
         cast_w1(1)
         quant_w1(1)
-        gather_q(3)
+        deal_scales()
+        gather_q(3, (0,))
         layer1(2, 0)
         layer1(2, 1)
         for c in range(NCH):
@@ -255,15 +261,27 @@ def tile_picked_expertpair_gelu_po_kernel(
                 layer1(2, c + 2)
         deal_words(2)
         deal_words(1)
-        for c in range(NCH):
+        hidden(0)
+        minus_b(0)
+        gather_q(3, (1,))
+        hidden(1)
+        for c in range(2, NCH):
             hidden(c)
-        for c in range(NCH):
+            minus_b(c - 1)
+        minus_b(NCH - 1)
+        mul(0)
+        sub(0)
+        mul(1)
+        for c in range(2, NCH):
             mul(c)
-            if c == NCH - 1:
-                quant_y(0)
-            sub(c)
-        for c in (2, 1, 3):
-            quant_y(c)
+            sub(c - 1)
+        sub(NCH - 1)
+        half = S // 2
+        quant_y(0, 2)
+        nc.sync.dma_start(o1[:, :half], o_c[:, :half])
+        quant_y(2, 3)
+        quant_y(3, 4)
+        nc.sync.dma_start(o1[:, half:], o_c[:, half:])
         for q in range(4):
             eng = nc.scalar if q % 2 else nc.sync
             eng.dma_start(out_2[0, 4 * q : 4 * q + 4, :].bitcast(I32), o_s[32 * q : 32 * q + 4, :].bitcast(I32))

@@ -20,7 +20,7 @@ PACK = 4
 CH = 128
 NCH = S // CH
 HALF = 256
-POOL_CHUNK = 0
+POOL_CHUNK = 1
 
 
 def tile_picked_expertpair_gelu_po_kernel(
@@ -63,14 +63,14 @@ def tile_picked_expertpair_gelu_po_kernel(
 
         nc.sync.dma_start(task_t[:], task)
         load_mix(0)
-        nc.sync.dma_start(offs_t[:], offs)
+        load_mix(1)
         for q in range(4):
             nc.sync.dma_start(xs[32 * q : 32 * q + 4, :].bitcast(I32), x_scales[0, 4 * q : 4 * q + 4, :].bitcast(I32))
         nc.sync.dma_start(w2_raw[:], w_rows[2])
-        load_mix(1)
-        load_ws(nc.sync, 2)
+        nc.sync.dma_start(offs_t[:], offs)
         load_mix(2)
         nc.sync.dma_start(w1_raw[0][:], w_rows[1][:, :, :HALF])
+        load_ws(nc.sync, 2)
         nc.sync.dma_start(xw[:], x_words[0].rearrange("p n t -> p (n t)").bitcast(I32))
         load_ws(nc.sync, 1)
         nc.sync.dma_start(w1_raw[1][:], w_rows[1][:, :, HALF:])
@@ -238,8 +238,8 @@ def tile_picked_expertpair_gelu_po_kernel(
             )
 
         gather_q(0)
-        nc.vector.tensor_copy(xg_s[:], xs[:].indirect(offs_t[:]))
         gather_q(1)
+        nc.vector.tensor_copy(xg_s[:], xs[:].indirect(offs_t[:]))
         cast_w2(0)
         cast_w2(1)
         gather_q(2)
@@ -262,20 +262,19 @@ def tile_picked_expertpair_gelu_po_kernel(
         deal_words(2)
         deal_words(1)
         hidden(0)
-        minus_b(0)
         gather_q(3, (1,))
         hidden(1)
+        minus_b(1)
+        minus_b(0)
         for c in range(2, NCH):
             hidden(c)
-            minus_b(c - 1)
-        minus_b(NCH - 1)
-        mul(0)
-        sub(0)
-        mul(1)
         for c in range(2, NCH):
-            mul(c)
-            sub(c - 1)
-        sub(NCH - 1)
+            minus_b(c)
+        for c0 in (0, 2):
+            mul(c0)
+            mul(c0 + 1)
+            sub(c0)
+            sub(c0 + 1)
         half = S // 2
         quant_y(0, 2)
         nc.sync.dma_start(o1[:, :half], o_c[:, :half])

@@ -52,9 +52,9 @@ def tile_picked_expertpair_gelu_po_kernel(
         def load_mix(t):
             nc.sync.dma_start(mix_t[t][:], mix_rows[:, t, :])
 
-        def load_ws(eng, n):
-            for q in range(4):
-                eng.dma_start(
+        def load_ws(n, quadrants):
+            for q in quadrants:
+                nc.sync.dma_start(
                     ws_raw[32 * q + 4 * n : 32 * q + 4 * n + 4, :].bitcast(I32), scales2[n][0, 4 * q : 4 * q + 4, :].bitcast(I32)
                 )
 
@@ -64,19 +64,16 @@ def tile_picked_expertpair_gelu_po_kernel(
         nc.sync.dma_start(task_t[:], task)
         load_mix(0)
         load_mix(1)
-        for q in range(4):
-            nc.sync.dma_start(xs[32 * q : 32 * q + 4, :].bitcast(I32), x_scales[0, 4 * q : 4 * q + 4, :].bitcast(I32))
+        nc.sync.dma_start(xs[0:P:8, :].bitcast(I32), x_scales[0].bitcast(I32))
+        load_ws(2, (0, 1, 2))
         nc.sync.dma_start(w2_raw[:], w_rows[2])
         nc.sync.dma_start(offs_t[:], offs)
         load_mix(2)
+        load_ws(2, (3,))
+        load_ws(1, (0, 1, 2))
         nc.sync.dma_start(w1_raw[0][:], w_rows[1][:, :, :HALF])
-        load_ws(nc.sync, 2)
+        load_ws(1, (3,))
         nc.sync.dma_start(xw[:], x_words[0].rearrange("p n t -> p (n t)").bitcast(I32))
-        load_ws(nc.sync, 1)
-        nc.sync.dma_start(w1_raw[1][:], w_rows[1][:, :, HALF:])
-        load_mix(3)
-        load_ww(2)
-        load_ww(1)
 
         q4 = keep.tile([P, PACK, S], F32, name="q4", align_bytes=64)
 
@@ -87,7 +84,9 @@ def tile_picked_expertpair_gelu_po_kernel(
                 )
 
         xg_w = [keep.tile([P, HALF], U32, name="xg_w%d" % h, align_bytes=64) for h in range(2)]
+        xg_rows = keep.tile([P, S], U8, name="xg_rows", align_bytes=64)
         xg_s = keep.tile([P, S], U8, name="xg_s", align_bytes=64)
+        nc.vector.memset(xg_s[:].bitcast(I32), 0)
         w_bf = {(n, h): keep.tile([P, 2 * H], BF16, name="w_bf%d%d" % (n, h), tag="w_bf%d%d" % (n, h), align_bytes=64) for n in (1, 2) for h in range(2)}
         w_c = {n: keep.tile([P, H], U32, name="w_c%d" % n, align_bytes=64) for n in (1, 2)}
         w_s = {n: keep.tile([P, H], U8, name="w_s%d" % n, align_bytes=64) for n in (1, 2)}
@@ -125,7 +124,7 @@ def tile_picked_expertpair_gelu_po_kernel(
             )
 
         def deal_scales():
-            ws = keep.tile([P, N], U8, name="ws", tag="w1_raw1", align_bytes=64)
+            ws = keep.tile([P, N], U8, name="ws", align_bytes=64)
             dealt["ws"] = ws
             nc.vector.tensor_copy(ws[:].rearrange("p (t m) -> p t m", t=PACK), ws_raw[:].rearrange("p (m t) -> p t m", t=PACK))
 
@@ -151,7 +150,7 @@ def tile_picked_expertpair_gelu_po_kernel(
             if (n, c) == (1, 0):
                 z_bf[n, c] = q4[:, PACK - 1, HALF:].bitcast(BF16)
             else:
-                z_bf[n, c] = keep.tile([P, CH * PACK], BF16, name="z_bf%d%d" % (n, c), align_bytes=64)[:]
+                z_bf[n, c] = keep.tile([P, CH * PACK], BF16, name="z_bf%d%d" % (n, c), tag="z_bf%d%d" % (n, c % 3 if n == 2 else c), align_bytes=64)[:]
             nc.scalar.activation(
                 z_bf[n, c].rearrange("p (s t) -> p s t", t=PACK), bank[:].rearrange("p t s -> p s t"), ACT.Gelu_apprx_tanh
             )
@@ -239,19 +238,25 @@ def tile_picked_expertpair_gelu_po_kernel(
 
         gather_q(0)
         gather_q(1)
-        nc.vector.tensor_copy(xg_s[:], xs[:].indirect(offs_t[:]))
+        nc.vector.tensor_copy(xg_rows[:], xs[:].indirect(offs_t[:]))
+        for r in range(4):
+            nc.sync.dma_start(xg_s[r:P:32, :].bitcast(I32), xg_rows[8 * r : P : 32, :].bitcast(I32))
+        nc.sync.dma_start(w1_raw[1][:], w_rows[1][:, :, HALF:])
+        load_mix(3)
+        load_ww(2)
+        load_ww(1)
         cast_w2(0)
         cast_w2(1)
         gather_q(2)
         quant_w2(0)
         quant_w2(1)
+        deal_scales()
         cast_w1(0)
         quant_w1(0)
         for h in range(2):
             nc.vector.tensor_copy(xg_w[h][:], xw[:].bitcast(U32).indirect(offs_t[:, h * 16 : (h + 1) * 16]))
         cast_w1(1)
         quant_w1(1)
-        deal_scales()
         gather_q(3, (0,))
         layer1(2, 0)
         layer1(2, 1)

@@ -21,6 +21,8 @@ CH = 128
 NCH = S // CH
 HALF = 256
 POOL_CHUNK = 1
+W2_SPLIT = 96
+W1_SPLIT = 48
 
 
 def tile_picked_expertpair_gelu_po_kernel(
@@ -33,16 +35,20 @@ def tile_picked_expertpair_gelu_po_kernel(
 
         offs_t = keep.tile([P, S // 16], U16, name="offs_t")
         task_t = keep.tile([P, S // 16], U16, name="task_t")
-        xw = keep.tile([P, T], I32, name="xw", align_bytes=64)
+        xw = keep.tile([P, T], I32, name="xw", tag="xw", align_bytes=64)
         xs = keep.tile([P, T], U8, name="xs", align_bytes=64)
         ws_raw = keep.tile([P, N], U8, name="ws_raw", align_bytes=64)
         ww_raw = {n: keep.tile([P, N], I32, name="ww_raw%d" % n, align_bytes=64) for n in (1, 2)}
         mix_t = [keep.tile([P, U], F32, name="mix%d" % t, align_bytes=64) for t in range(PACK)]
-        w2_raw = keep.tile([P, PACK, H], F32, name="w2_raw", align_bytes=64)
-        w1_raw = [keep.tile([P, PACK, HALF], F32, name="w1_raw%d" % h, tag="w1_raw%d" % h, align_bytes=64) for h in range(2)]
+        w_raw = {n: keep.tile([P, PACK, H], F32, name="w_raw%d" % n, tag="w_raw%d" % n, align_bytes=64) for n in (1, 2)}
+        xg_w = [keep.tile([P, HALF], U32, name="xg_w%d" % h, align_bytes=64) for h in range(2)]
+        xg_rows = keep.tile([P, S], U8, name="xg_rows", align_bytes=64)
+        xg_s = keep.tile([P, S], U8, name="xg_s", align_bytes=64)
+        q4 = keep.tile([P, PACK, S], F32, name="q4", align_bytes=64)
 
         nc.vector.memset(xs[:].bitcast(I32), 0)
         nc.vector.memset(ws_raw[:].bitcast(I32), 0)
+        nc.vector.memset(xg_s[:].bitcast(I32), 0)
 
         mix_rows = mix.rearrange("(p t) u -> p t u", t=PACK)
         w_rows = {1: w1.rearrange("(p j) c -> p j c", j=PACK), 2: w2.rearrange("(p j) c -> p j c", j=PACK)}
@@ -61,58 +67,29 @@ def tile_picked_expertpair_gelu_po_kernel(
         def load_ww(n):
             nc.sync.dma_start(ww_raw[n][:], words2[n][0].rearrange("p n t -> p (n t)").bitcast(I32))
 
-        nc.sync.dma_start(task_t[:], task)
-        load_mix(0)
-        load_mix(1)
-        nc.sync.dma_start(xs[0:P:8, :].bitcast(I32), x_scales[0].bitcast(I32))
-        load_ws(2, (0, 1, 2))
-        nc.sync.dma_start(w2_raw[:], w_rows[2])
-        nc.sync.dma_start(offs_t[:], offs)
-        load_mix(2)
-        load_ws(2, (3,))
-        load_ws(1, (0, 1, 2))
-        nc.sync.dma_start(w1_raw[0][:], w_rows[1][:, :, :HALF])
-        load_ws(1, (3,))
-        nc.sync.dma_start(xw[:], x_words[0].rearrange("p n t -> p (n t)").bitcast(I32))
-
-        q4 = keep.tile([P, PACK, S], F32, name="q4", align_bytes=64)
-
         def gather_q(t, halves=(0, 1)):
             for h in halves:
                 nc.vector.tensor_copy(
                     q4[:, t, h * HALF : (h + 1) * HALF], mix_t[t][:].indirect(task_t[:, h * 16 : (h + 1) * 16])
                 )
 
-        xg_w = [keep.tile([P, HALF], U32, name="xg_w%d" % h, align_bytes=64) for h in range(2)]
-        xg_rows = keep.tile([P, S], U8, name="xg_rows", align_bytes=64)
-        xg_s = keep.tile([P, S], U8, name="xg_s", align_bytes=64)
-        nc.vector.memset(xg_s[:].bitcast(I32), 0)
-        w_bf = {(n, h): keep.tile([P, 2 * H], BF16, name="w_bf%d%d" % (n, h), tag="w_bf%d%d" % (n, h), align_bytes=64) for n in (1, 2) for h in range(2)}
+        w_bf = {n: keep.tile([P, PACK * H], BF16, name="w_bf%d" % n, tag="w_bf%d" % n, align_bytes=64) for n in (1, 2)}
         w_c = {n: keep.tile([P, H], U32, name="w_c%d" % n, align_bytes=64) for n in (1, 2)}
         w_s = {n: keep.tile([P, H], U8, name="w_s%d" % n, align_bytes=64) for n in (1, 2)}
 
-        def cast_w2(h):
-            dst = w_bf[2, h][:].rearrange("p (t m j) -> p m j t", t=2, j=PACK)
-            nc.scalar.copy(dst, w2_raw[:].rearrange("p j (m t) -> p m j t", t=PACK)[:, :, :, 2 * h : 2 * h + 2])
-
-        def quant_w2(h):
-            cols = slice(h * HALF, (h + 1) * HALF)
-            nc.vector.quantize_mx(out=w_c[2][:, cols].bitcast(FP8X4), scales=w_s[2][:, cols], in_=w_bf[2, h][:])
-
-        def cast_w1(h):
-            dst = w_bf[1, h][:].rearrange("p (t m j) -> p m j t", t=PACK, j=PACK)
-            src = w1_raw[h][:].rearrange("p j (m t) -> p m j t", t=PACK)
-            if h:
+        def cast_w(n, on_vector, ms, ts):
+            dst = w_bf[n][:].rearrange("p (t m j) -> p m j t", t=PACK, j=PACK)[:, ms, :, ts]
+            src = w_raw[n][:].rearrange("p j (m t) -> p m j t", t=PACK)[:, ms, :, ts]
+            if on_vector:
                 nc.vector.tensor_copy(dst.rearrange("p m j t -> p m t j"), src.rearrange("p m j t -> p m t j"))
             else:
                 nc.scalar.copy(dst, src)
 
-        def quant_w1(h):
-            for t in range(PACK):
-                cols = slice(t * P + h * 64, t * P + (h + 1) * 64)
-                nc.vector.quantize_mx(
-                    out=w_c[1][:, cols].bitcast(FP8X4), scales=w_s[1][:, cols], in_=w_bf[1, h][:, t * HALF : (t + 1) * HALF]
-                )
+        def quant_w(n, h):
+            cols = slice(h * HALF, (h + 1) * HALF)
+            nc.vector.quantize_mx(
+                out=w_c[n][:, cols].bitcast(FP8X4), scales=w_s[n][:, cols], in_=w_bf[n][:, h * HALF * PACK : (h + 1) * HALF * PACK]
+            )
 
         ww = {n: keep.tile([P, N], U32, name="ww%d" % n, align_bytes=64) for n in (1, 2)}
         dealt = {}
@@ -147,20 +124,16 @@ def tile_picked_expertpair_gelu_po_kernel(
                     start=True,
                     stop=True,
                 )
-            if (n, c) == (1, 0):
-                z_bf[n, c] = q4[:, PACK - 1, HALF:].bitcast(BF16)
-            else:
-                z_bf[n, c] = keep.tile([P, CH * PACK], BF16, name="z_bf%d%d" % (n, c), tag="z_bf%d%d" % (n, c % 3 if n == 2 else c), align_bytes=64)[:]
-            nc.scalar.activation(
-                z_bf[n, c].rearrange("p (s t) -> p s t", t=PACK), bank[:].rearrange("p t s -> p s t"), ACT.Gelu_apprx_tanh
-            )
+            return bank
+
+        def gelu(n, c, bank, dst):
+            z_bf[n, c] = dst
+            nc.scalar.activation(dst.rearrange("p (s t) -> p s t", t=PACK), bank[:].rearrange("p t s -> p s t"), ACT.Gelu_apprx_tanh)
 
         nz = {}
 
         def negate(c):
-            if c == 0:
-                nz["tile"] = keep.tile([P, S * PACK], BF16, name="nz", tag="w_bf11", align_bytes=64)
-            nz[c] = nz["tile"][:, c * CH * PACK : (c + 1) * CH * PACK]
+            nz[c] = nz["tile"][:, c, :]
             nc.vector.tensor_scalar_mul(nz[c], z_bf[2, c], -1.0)
 
         def quant_z(n, c):
@@ -186,12 +159,11 @@ def tile_picked_expertpair_gelu_po_kernel(
         diff = {}
         nb_sb = {}
 
-        def hidden(c):
-            negate(c)
-            quant_z(2, c)
+        def diff_b(c):
             diff[c] = psum.tile([P, PACK, CH], F32, name="diff%d" % c, tag="bank2%d" % c)
             passes2(diff[c], 2, c, True, False, False)
-            quant_z(1, c)
+
+        def diff_a(c):
             passes2(diff[c], 1, c, False, True, False)
 
         def minus_b(c):
@@ -236,43 +208,76 @@ def tile_picked_expertpair_gelu_po_kernel(
                 out=o_c[:, cols].bitcast(FP8X4), scales=o_s[:, cols], in_=y_bf[:, first * CH * PACK : last * CH * PACK]
             )
 
+        nc.sync.dma_start(task_t[:], task)
+        load_mix(0)
+        nc.sync.dma_start(offs_t[:], offs)
+        nc.sync.dma_start(xs[0:P:8, :].bitcast(I32), x_scales[0].bitcast(I32))
+        load_mix(1)
+        load_ws(2, (0, 1))
+        nc.sync.dma_start(w_raw[2][:], w_rows[2])
+        load_mix(2)
+        load_ws(2, (2, 3))
+        load_ws(1, (0, 1, 2))
+        nc.sync.dma_start(xw[:], x_words[0].rearrange("p n t -> p (n t)").bitcast(I32))
+
         gather_q(0)
-        gather_q(1)
         nc.vector.tensor_copy(xg_rows[:], xs[:].indirect(offs_t[:]))
+        gather_q(1)
+        load_mix(3)
+        load_ws(1, (3,))
         for r in range(4):
             nc.sync.dma_start(xg_s[r:P:32, :].bitcast(I32), xg_rows[8 * r : P : 32, :].bitcast(I32))
-        nc.sync.dma_start(w1_raw[1][:], w_rows[1][:, :, HALF:])
-        load_mix(3)
+        nc.sync.dma_start(w_raw[1][:], w_rows[1])
         load_ww(2)
         load_ww(1)
-        cast_w2(0)
-        cast_w2(1)
+        cast_w(2, False, slice(0, P), slice(0, 2))
+        cast_w(2, False, slice(0, W2_SPLIT), slice(2, 4))
+        cast_w(2, True, slice(W2_SPLIT, P), slice(2, 4))
         gather_q(2)
-        quant_w2(0)
-        quant_w2(1)
-        deal_scales()
-        cast_w1(0)
-        quant_w1(0)
+        quant_w(2, 0)
+        quant_w(2, 1)
         for h in range(2):
             nc.vector.tensor_copy(xg_w[h][:], xw[:].bitcast(U32).indirect(offs_t[:, h * 16 : (h + 1) * 16]))
-        cast_w1(1)
-        quant_w1(1)
-        gather_q(3, (0,))
-        layer1(2, 0)
-        layer1(2, 1)
+        gather_q(3)
+        deal_scales()
+        hid = {(2, c): layer1(2, c) for c in range(NCH)}
+        z20 = keep.tile([P, CH * PACK], BF16, name="z20", align_bytes=64)
+        z21 = keep.tile([P, CH * PACK], BF16, name="z21", align_bytes=64)
+        gelu(2, 0, hid[2, 0], z20[:])
+        gelu(2, 1, hid[2, 1], z21[:])
+        cast_w(1, False, slice(W1_SPLIT, P), slice(2, 4))
+        cast_w(1, True, slice(0, P), slice(0, 2))
+        cast_w(1, True, slice(0, W1_SPLIT), slice(2, 4))
+        quant_w(1, 0)
+        quant_w(1, 1)
         for c in range(NCH):
-            layer1(1, c)
-            if c + 2 < NCH:
-                layer1(2, c + 2)
+            hid[1, c] = layer1(1, c)
+        z2r = keep.tile([P, NCH + 2, CH * PACK], BF16, name="z2r", tag="w_raw1", align_bytes=64)
+        nz["tile"] = z2r
+        z1 = keep.tile([P, NCH, CH * PACK], BF16, name="z1", align_bytes=64)
+        gelu(2, 2, hid[2, 2], z2r[:, NCH, :])
+        gelu(2, 3, hid[2, 3], z2r[:, NCH + 1, :])
+        gelu(1, 0, hid[1, 0], z1[:, 3, :])
+        gelu(1, 1, hid[1, 1], z1[:, 0, :])
+        gelu(1, 2, hid[1, 2], z1[:, 1, :])
+        gelu(1, 3, hid[1, 3], z1[:, 2, :])
+        negate(0)
+        negate(1)
         deal_words(2)
+        quant_z(2, 0)
+        quant_z(2, 1)
         deal_words(1)
-        hidden(0)
-        gather_q(3, (1,))
-        hidden(1)
-        minus_b(1)
-        minus_b(0)
-        for c in range(2, NCH):
-            hidden(c)
+        negate(2)
+        negate(3)
+        for c in range(NCH):
+            if c > 1:
+                quant_z(2, c)
+            diff_b(c)
+            quant_z(1, c)
+            diff_a(c)
+            if c == 1:
+                minus_b(1)
+                minus_b(0)
         for c in range(2, NCH):
             minus_b(c)
         for c0 in (0, 2):

@@ -112,7 +112,7 @@ def tile_picked_expertpair_gelu_po_kernel(
         def layer1(n, c):
             cols = slice(c * CH, (c + 1) * CH)
             gcols = slice(c % 2 * CH, (c % 2 + 1) * CH)
-            bank = psum.tile([P, PACK, CH], F32, name="hid%d%d" % (n, c), tag="bank%d%d" % (n, c))
+            bank = psum.tile([P, PACK, CH], F32, name="hid%d%d" % (n, c), tag="bank%d%d" % (n, c % 2 if n == 2 else c))
             for t in range(PACK):
                 tc_ = slice(t * P, (t + 1) * P)
                 nc.tensor.matmul_mx(
@@ -160,7 +160,7 @@ def tile_picked_expertpair_gelu_po_kernel(
         nb_sb = {}
 
         def diff_b(c):
-            diff[c] = psum.tile([P, PACK, CH], F32, name="diff%d" % c, tag="bank2%d" % c)
+            diff[c] = psum.tile([P, PACK, CH], F32, name="diff%d" % c, tag="bank2%d" % ((c + 2) % NCH))
             passes2(diff[c], 2, c, True, False, False)
 
         def diff_a(c):
@@ -210,9 +210,9 @@ def tile_picked_expertpair_gelu_po_kernel(
 
         nc.sync.dma_start(task_t[:], task)
         load_mix(0)
+        load_mix(1)
         nc.sync.dma_start(offs_t[:], offs)
         nc.sync.dma_start(xs[0:P:8, :].bitcast(I32), x_scales[0].bitcast(I32))
-        load_mix(1)
         load_ws(2, (0, 1))
         nc.sync.dma_start(w_raw[2][:], w_rows[2])
         load_mix(2)
@@ -221,8 +221,8 @@ def tile_picked_expertpair_gelu_po_kernel(
         nc.sync.dma_start(xw[:], x_words[0].rearrange("p n t -> p (n t)").bitcast(I32))
 
         gather_q(0)
-        nc.vector.tensor_copy(xg_rows[:], xs[:].indirect(offs_t[:]))
         gather_q(1)
+        nc.vector.tensor_copy(xg_rows[:], xs[:].indirect(offs_t[:]))
         load_mix(3)
         load_ws(1, (3,))
         for r in range(4):
@@ -240,11 +240,13 @@ def tile_picked_expertpair_gelu_po_kernel(
             nc.vector.tensor_copy(xg_w[h][:], xw[:].bitcast(U32).indirect(offs_t[:, h * 16 : (h + 1) * 16]))
         gather_q(3)
         deal_scales()
-        hid = {(2, c): layer1(2, c) for c in range(NCH)}
+        hid = {(2, c): layer1(2, c) for c in range(2)}
         z20 = keep.tile([P, CH * PACK], BF16, name="z20", align_bytes=64)
         z21 = keep.tile([P, CH * PACK], BF16, name="z21", align_bytes=64)
         gelu(2, 0, hid[2, 0], z20[:])
         gelu(2, 1, hid[2, 1], z21[:])
+        for c in range(2, NCH):
+            hid[2, c] = layer1(2, c)
         cast_w(1, False, slice(W1_SPLIT, P), slice(2, 4))
         cast_w(1, True, slice(0, P), slice(0, 2))
         cast_w(1, True, slice(0, W1_SPLIT), slice(2, 4))

@@ -22,7 +22,7 @@ NCH = S // CH
 HALF = 256
 POOL_CHUNK = 1
 W2_SPLIT = 96
-W1_SPLIT = 48
+W1_SPLIT = 88
 
 
 def tile_picked_expertpair_gelu_po_kernel(
@@ -77,9 +77,9 @@ def tile_picked_expertpair_gelu_po_kernel(
         w_c = {n: keep.tile([P, H], U32, name="w_c%d" % n, align_bytes=64) for n in (1, 2)}
         w_s = {n: keep.tile([P, H], U8, name="w_s%d" % n, align_bytes=64) for n in (1, 2)}
 
-        def cast_w(n, on_vector, ms, ts):
-            dst = w_bf[n][:].rearrange("p (t m j) -> p m j t", t=PACK, j=PACK)[:, ms, :, ts]
-            src = w_raw[n][:].rearrange("p j (m t) -> p m j t", t=PACK)[:, ms, :, ts]
+        def cast_w(n, on_vector, ms):
+            dst = w_bf[n][:].rearrange("p (t m j) -> p m j t", t=PACK, j=PACK)[:, ms]
+            src = w_raw[n][:].rearrange("p j (m t) -> p m j t", t=PACK)[:, ms]
             if on_vector:
                 nc.vector.tensor_copy(dst.rearrange("p m j t -> p m t j"), src.rearrange("p m j t -> p m t j"))
             else:
@@ -160,14 +160,14 @@ def tile_picked_expertpair_gelu_po_kernel(
         nb_sb = {}
 
         def diff_b(c):
-            diff[c] = psum.tile([P, PACK, CH], F32, name="diff%d" % c, tag="bank2%d" % ((c + 2) % NCH))
+            diff[c] = psum.tile([P, PACK, CH], F32, name="diff%d" % c, tag=("bank22", "bank23", "bank12", "bank13")[c])
             passes2(diff[c], 2, c, True, False, False)
 
         def diff_a(c):
             passes2(diff[c], 1, c, False, True, False)
 
         def minus_b(c):
-            nb[c] = psum.tile([P, PACK, CH], F32, name="nb%d" % c, tag="bank1%d" % c)
+            nb[c] = psum.tile([P, PACK, CH], F32, name="nb%d" % c, tag=("bank11", "bank21", "bank22", "bank23")[c])
             passes2(nb[c], 2, c, False, False, True)
             if c == POOL_CHUNK:
                 nb_sb[c] = keep.tile([P, PACK, CH], F32, name="nb_sb%d" % c, align_bytes=64)
@@ -208,8 +208,8 @@ def tile_picked_expertpair_gelu_po_kernel(
                 out=o_c[:, cols].bitcast(FP8X4), scales=o_s[:, cols], in_=y_bf[:, first * CH * PACK : last * CH * PACK]
             )
 
-        nc.sync.dma_start(task_t[:], task)
         load_mix(0)
+        nc.sync.dma_start(task_t[:], task)
         load_mix(1)
         nc.sync.dma_start(offs_t[:], offs)
         nc.sync.dma_start(xs[0:P:8, :].bitcast(I32), x_scales[0].bitcast(I32))
@@ -230,9 +230,8 @@ def tile_picked_expertpair_gelu_po_kernel(
         nc.sync.dma_start(w_raw[1][:], w_rows[1])
         load_ww(2)
         load_ww(1)
-        cast_w(2, False, slice(0, P), slice(0, 2))
-        cast_w(2, False, slice(0, W2_SPLIT), slice(2, 4))
-        cast_w(2, True, slice(W2_SPLIT, P), slice(2, 4))
+        cast_w(2, False, slice(0, W2_SPLIT))
+        cast_w(2, True, slice(W2_SPLIT, P))
         gather_q(2)
         quant_w(2, 0)
         quant_w(2, 1)
@@ -247,9 +246,9 @@ def tile_picked_expertpair_gelu_po_kernel(
         gelu(2, 1, hid[2, 1], z21[:])
         for c in range(2, NCH):
             hid[2, c] = layer1(2, c)
-        cast_w(1, False, slice(W1_SPLIT, P), slice(2, 4))
-        cast_w(1, True, slice(0, P), slice(0, 2))
-        cast_w(1, True, slice(0, W1_SPLIT), slice(2, 4))
+        cast_w(1, False, slice(W1_SPLIT, P))
+        cast_w(1, True, slice(0, W1_SPLIT))
+        deal_words(2)
         quant_w(1, 0)
         quant_w(1, 1)
         for c in range(NCH):
@@ -265,10 +264,9 @@ def tile_picked_expertpair_gelu_po_kernel(
         gelu(1, 3, hid[1, 3], z1[:, 2, :])
         negate(0)
         negate(1)
-        deal_words(2)
+        deal_words(1)
         quant_z(2, 0)
         quant_z(2, 1)
-        deal_words(1)
         negate(2)
         negate(3)
         for c in range(NCH):
@@ -280,11 +278,11 @@ def tile_picked_expertpair_gelu_po_kernel(
             if c == 1:
                 minus_b(1)
                 minus_b(0)
-        for c in range(2, NCH):
-            minus_b(c)
         for c0 in (0, 2):
-            mul(c0)
-            mul(c0 + 1)
+            for c in (c0, c0 + 1):
+                mul(c)
+                if c0 == 0:
+                    minus_b(c + 2)
             sub(c0)
             sub(c0 + 1)
         half = S // 2

@@ -22,7 +22,7 @@ NCH = S // CH
 HALF = 256
 POOL_CHUNK = 1
 W2_SPLIT = 96
-W1_SPLIT = 88
+W1_SPLIT = 80
 
 
 def tile_picked_expertpair_gelu_po_kernel(
@@ -73,7 +73,8 @@ def tile_picked_expertpair_gelu_po_kernel(
                     q4[:, t, h * HALF : (h + 1) * HALF], mix_t[t][:].indirect(task_t[:, h * 16 : (h + 1) * 16])
                 )
 
-        w_bf = {n: keep.tile([P, PACK * H], BF16, name="w_bf%d" % n, tag="w_bf%d" % n, align_bytes=64) for n in (1, 2)}
+        w_bf = {2: keep.tile([P, PACK * H], BF16, name="w_bf2", align_bytes=64)}
+        w1_bf = [keep.tile([P, PACK * HALF], BF16, name="w1_bf%d" % h, tag="w1_bf%d" % h, align_bytes=64) for h in range(2)]
         w_c = {n: keep.tile([P, H], U32, name="w_c%d" % n, align_bytes=64) for n in (1, 2)}
         w_s = {n: keep.tile([P, H], U8, name="w_s%d" % n, align_bytes=64) for n in (1, 2)}
 
@@ -91,10 +92,27 @@ def tile_picked_expertpair_gelu_po_kernel(
                 out=w_c[n][:, cols].bitcast(FP8X4), scales=w_s[n][:, cols], in_=w_bf[n][:, h * HALF * PACK : (h + 1) * HALF * PACK]
             )
 
-        ww = {n: keep.tile([P, N], U32, name="ww%d" % n, align_bytes=64) for n in (1, 2)}
+        def cast_w1(on_vector, first, last):
+            h = first // 64
+            dst = w1_bf[h][:].rearrange("p (t m j) -> p m j t", t=PACK, j=PACK)[:, first - 64 * h : last - 64 * h]
+            src = w_raw[1][:].rearrange("p j (m t) -> p m j t", t=PACK)[:, first:last]
+            if on_vector:
+                nc.vector.tensor_copy(dst.rearrange("p m j t -> p m t j"), src.rearrange("p m j t -> p m t j"))
+            else:
+                nc.scalar.copy(dst, src)
+
+        def quant_w1(h):
+            for t in range(PACK):
+                cols = slice(t * P + h * 64, t * P + (h + 1) * 64)
+                nc.vector.quantize_mx(
+                    out=w_c[1][:, cols].bitcast(FP8X4), scales=w_s[1][:, cols], in_=w1_bf[h][:, t * HALF : (t + 1) * HALF]
+                )
+
+        ww = {}
         dealt = {}
 
         def deal_words(n):
+            ww[n] = keep.tile([P, N], U32, name="ww%d" % n, tag="w1_bf0" if n == 2 else "ww1", align_bytes=64)
             nc.vector.tensor_copy(
                 ww[n][:].rearrange("p (t g i) -> p g t i", t=PACK, i=4),
                 ww_raw[n][:].bitcast(U32).rearrange("p (g i t) -> p g t i", t=PACK, i=4),
@@ -160,14 +178,14 @@ def tile_picked_expertpair_gelu_po_kernel(
         nb_sb = {}
 
         def diff_b(c):
-            diff[c] = psum.tile([P, PACK, CH], F32, name="diff%d" % c, tag=("bank22", "bank23", "bank12", "bank13")[c])
+            diff[c] = psum.tile([P, PACK, CH], F32, name="diff%d" % c, tag=("bank22", "bank23", "bank13", "bank22")[c])
             passes2(diff[c], 2, c, True, False, False)
 
         def diff_a(c):
             passes2(diff[c], 1, c, False, True, False)
 
         def minus_b(c):
-            nb[c] = psum.tile([P, PACK, CH], F32, name="nb%d" % c, tag=("bank11", "bank21", "bank22", "bank23")[c])
+            nb[c] = psum.tile([P, PACK, CH], F32, name="nb%d" % c, tag=("bank12", "bank11", "bank23", "bank11")[c])
             passes2(nb[c], 2, c, False, False, True)
             if c == POOL_CHUNK:
                 nb_sb[c] = keep.tile([P, PACK, CH], F32, name="nb_sb%d" % c, align_bytes=64)
@@ -179,22 +197,24 @@ def tile_picked_expertpair_gelu_po_kernel(
         o1 = out_1[0].rearrange("p n t -> p (n t)").bitcast(I32)
         prod = {}
         y = {}
-        y_bf = keep.tile([P, S * PACK], BF16, name="y_bf", align_bytes=64)
+        y_bf = {}
 
         def mul(c):
             cols = slice(c * CH, (c + 1) * CH)
-            prod[c] = keep.tile([P, PACK, CH], F32, name="prod%d" % c, align_bytes=64)
+            prod[c] = keep.tile([P, PACK, CH], F32, name="prod%d" % c, tag="prod%d" % c, align_bytes=64)
             nc.vector.tensor_tensor(prod[c][:], diff[c][:], q4[:, :, cols], ALU.mult)
 
         def sub(c):
             cols = slice(c * CH, (c + 1) * CH)
-            y[c] = keep.tile([P, PACK, CH], F32, name="y%d" % c, align_bytes=64)
+            y[c] = keep.tile([P, PACK, CH], F32, name="y%d" % c, tag="z1" if c == POOL_CHUNK else "y%d" % c, align_bytes=64)
             if c == POOL_CHUNK:
                 nc.gpsimd.tensor_tensor(y[c][:], prod[c][:], nb_sb[c][:], ALU.subtract)
             else:
                 nc.vector.tensor_tensor(y[c][:], prod[c][:], nb[c][:], ALU.subtract)
             nc.sync.dma_start(out_rows[:, :, cols], y[c][:])
-            dst = y_bf[:, c * CH * PACK : (c + 1) * CH * PACK].rearrange("p (g i t) -> p g t i", i=4, t=PACK)
+            if c % 2 == 0:
+                y_bf[c // 2] = keep.tile([P, 2 * CH * PACK], BF16, name="y_bf%d" % c, tag="prod0" if c == 0 else "y_bf", align_bytes=64)
+            dst = y_bf[c // 2][:, c % 2 * CH * PACK : (c % 2 + 1) * CH * PACK].rearrange("p (g i t) -> p g t i", i=4, t=PACK)
             src = y[c][:].rearrange("p t (g i) -> p g t i", i=4)
             if c < NCH - 1:
                 nc.scalar.copy(dst, src)
@@ -205,7 +225,7 @@ def tile_picked_expertpair_gelu_po_kernel(
         def quant_y(first, last):
             cols = slice(first * CH, last * CH)
             nc.vector.quantize_mx(
-                out=o_c[:, cols].bitcast(FP8X4), scales=o_s[:, cols], in_=y_bf[:, first * CH * PACK : last * CH * PACK]
+                out=o_c[:, cols].bitcast(FP8X4), scales=o_s[:, cols], in_=y_bf[first // 2][:, first % 2 * CH * PACK : (last - first // 2 * 2) * CH * PACK]
             )
 
         load_mix(0)
@@ -246,16 +266,16 @@ def tile_picked_expertpair_gelu_po_kernel(
         gelu(2, 1, hid[2, 1], z21[:])
         for c in range(2, NCH):
             hid[2, c] = layer1(2, c)
-        cast_w(1, False, slice(W1_SPLIT, P))
-        cast_w(1, True, slice(0, W1_SPLIT))
-        deal_words(2)
-        quant_w(1, 0)
-        quant_w(1, 1)
+        cast_w1(False, W1_SPLIT, P)
+        cast_w1(True, 0, 64)
+        cast_w1(True, 64, W1_SPLIT)
+        quant_w1(0)
+        quant_w1(1)
         for c in range(NCH):
             hid[1, c] = layer1(1, c)
         z2r = keep.tile([P, NCH + 2, CH * PACK], BF16, name="z2r", tag="w_raw1", align_bytes=64)
         nz["tile"] = z2r
-        z1 = keep.tile([P, NCH, CH * PACK], BF16, name="z1", align_bytes=64)
+        z1 = keep.tile([P, NCH, CH * PACK], BF16, name="z1", tag="z1", align_bytes=64)
         gelu(2, 2, hid[2, 2], z2r[:, NCH, :])
         gelu(2, 3, hid[2, 3], z2r[:, NCH + 1, :])
         gelu(1, 0, hid[1, 0], z1[:, 3, :])
@@ -264,27 +284,33 @@ def tile_picked_expertpair_gelu_po_kernel(
         gelu(1, 3, hid[1, 3], z1[:, 2, :])
         negate(0)
         negate(1)
-        deal_words(1)
+        deal_words(2)
         quant_z(2, 0)
         quant_z(2, 1)
-        negate(2)
-        negate(3)
-        for c in range(NCH):
-            if c > 1:
-                quant_z(2, c)
+        deal_words(1)
+        for c in range(2):
             diff_b(c)
             quant_z(1, c)
             diff_a(c)
-            if c == 1:
-                minus_b(1)
-                minus_b(0)
-        for c0 in (0, 2):
-            for c in (c0, c0 + 1):
-                mul(c)
-                if c0 == 0:
-                    minus_b(c + 2)
-            sub(c0)
-            sub(c0 + 1)
+        minus_b(1)
+        minus_b(0)
+        for c in range(2, NCH):
+            negate(c)
+        for c in range(2, NCH):
+            quant_z(2, c)
+        mul(0)
+        for c in range(2, NCH):
+            quant_z(1, c)
+            diff_b(c)
+            diff_a(c)
+        mul(1)
+        sub(0)
+        sub(1)
+        for c in range(2, NCH):
+            minus_b(c)
+            mul(c)
+        for c in range(2, NCH):
+            sub(c)
         half = S // 2
         quant_y(0, 2)
         nc.sync.dma_start(o1[:, :half], o_c[:, :half])

@@ -22,7 +22,7 @@ NCH = S // CH
 HALF = 256
 POOL_CHUNK = 1
 W2_SPLIT = 96
-W1_SPLIT = 80
+W1_SPLIT = 92
 
 
 def tile_picked_expertpair_gelu_po_kernel(
@@ -146,13 +146,16 @@ def tile_picked_expertpair_gelu_po_kernel(
 
         def gelu(n, c, bank, dst):
             z_bf[n, c] = dst
-            nc.scalar.activation(dst.rearrange("p (s t) -> p s t", t=PACK), bank[:].rearrange("p t s -> p s t"), ACT.Gelu_apprx_tanh)
+            if len(dst.shape) == 3:
+                nc.scalar.activation(dst.rearrange("p a (s t) -> p a s t", t=PACK), bank[:].rearrange("p t (a s) -> p a s t", a=2), ACT.Gelu_apprx_tanh)
+            else:
+                nc.scalar.activation(dst.rearrange("p (s t) -> p s t", t=PACK), bank[:].rearrange("p t s -> p s t"), ACT.Gelu_apprx_tanh)
 
         nz = {}
 
         def negate(c):
             nz[c] = nz["tile"][:, c, :]
-            nc.vector.tensor_scalar_mul(nz[c], z_bf[2, c], -1.0)
+            nc.vector.tensor_scalar_mul(nz[c].rearrange("p (a x) -> p a x", a=2) if c > 1 else nz[c], z_bf[2, c], -1.0)
 
         def quant_z(n, c):
             z_c[n, c] = keep.tile([P, CH], U32, name="z_c%d%d" % (n, c), align_bytes=64)
@@ -160,17 +163,18 @@ def tile_picked_expertpair_gelu_po_kernel(
             src = nz[c] if n == 2 else z_bf[1, c]
             nc.vector.quantize_mx(out=z_c[n, c][:].bitcast(FP8X4), scales=z_s[n, c][:], in_=src)
 
-        def passes2(bank, n, c, opens, closes, lone):
+        def passes2(banks, n, c, opens, closes, lone):
+            per = PACK // len(banks)
             for t in range(PACK):
                 tc_ = slice(t * P, (t + 1) * P)
                 nc.tensor.matmul_mx(
-                    out=bank[:, t, :],
+                    out=banks[t // per][:, t % per, :],
                     lhsT=ww[n][:, tc_].bitcast(FP8X4),
                     lhsT_scale=dealt["ws"][4 * n : P, tc_],
                     rhs=z_c[n, c][:].bitcast(FP8X4),
                     rhs_scale=z_s[n, c][:],
-                    start=lone or (opens and t == 0),
-                    stop=lone or (closes and t == PACK - 1),
+                    start=lone or (opens and t % per == 0),
+                    stop=lone or (closes and t % per == per - 1),
                 )
 
         nb = {}
@@ -178,15 +182,16 @@ def tile_picked_expertpair_gelu_po_kernel(
         nb_sb = {}
 
         def diff_b(c):
-            diff[c] = psum.tile([P, PACK, CH], F32, name="diff%d" % c, tag=("bank22", "bank23", "bank13", "bank22")[c])
+            tags = (("bank22", "bank20"), ("bank23",), ("bank13",), ("bank22",))[c]
+            diff[c] = [psum.tile([P, PACK // len(tags), CH], F32, name="diff%d%s" % (c, tag), tag=tag) for tag in tags]
             passes2(diff[c], 2, c, True, False, False)
 
         def diff_a(c):
             passes2(diff[c], 1, c, False, True, False)
 
         def minus_b(c):
-            nb[c] = psum.tile([P, PACK, CH], F32, name="nb%d" % c, tag=("bank12", "bank11", "bank23", "bank11")[c])
-            passes2(nb[c], 2, c, False, False, True)
+            nb[c] = psum.tile([P, PACK, CH], F32, name="nb%d" % c, tag=("bank12", "bank11", "bank12", "bank13")[c])
+            passes2([nb[c]], 2, c, False, False, True)
             if c == POOL_CHUNK:
                 nb_sb[c] = keep.tile([P, PACK, CH], F32, name="nb_sb%d" % c, align_bytes=64)
                 nc.scalar.copy(nb_sb[c][:], nb[c][:])
@@ -202,7 +207,10 @@ def tile_picked_expertpair_gelu_po_kernel(
         def mul(c):
             cols = slice(c * CH, (c + 1) * CH)
             prod[c] = keep.tile([P, PACK, CH], F32, name="prod%d" % c, tag="prod%d" % c, align_bytes=64)
-            nc.vector.tensor_tensor(prod[c][:], diff[c][:], q4[:, :, cols], ALU.mult)
+            per = PACK // len(diff[c])
+            for i, bank in enumerate(diff[c]):
+                ts = slice(i * per, (i + 1) * per)
+                nc.vector.tensor_tensor(prod[c][:, ts, :], bank[:], q4[:, ts, cols], ALU.mult)
 
         def sub(c):
             cols = slice(c * CH, (c + 1) * CH)
@@ -273,18 +281,17 @@ def tile_picked_expertpair_gelu_po_kernel(
         quant_w1(1)
         for c in range(NCH):
             hid[1, c] = layer1(1, c)
-        z2r = keep.tile([P, NCH + 2, CH * PACK], BF16, name="z2r", tag="w_raw1", align_bytes=64)
-        nz["tile"] = z2r
+        nz["tile"] = keep.tile([P, NCH, CH * PACK], BF16, name="nz", tag="w1_bf1", align_bytes=64)
         z1 = keep.tile([P, NCH, CH * PACK], BF16, name="z1", tag="z1", align_bytes=64)
-        gelu(2, 2, hid[2, 2], z2r[:, NCH, :])
-        gelu(2, 3, hid[2, 3], z2r[:, NCH + 1, :])
+        for c in range(2, NCH):
+            gelu(2, c, hid[2, c], w_raw[1][:, 2 * c - 4 : 2 * c - 2, H - CH :].bitcast(BF16))
         gelu(1, 0, hid[1, 0], z1[:, 3, :])
         gelu(1, 1, hid[1, 1], z1[:, 0, :])
         gelu(1, 2, hid[1, 2], z1[:, 1, :])
         gelu(1, 3, hid[1, 3], z1[:, 2, :])
+        deal_words(2)
         negate(0)
         negate(1)
-        deal_words(2)
         quant_z(2, 0)
         quant_z(2, 1)
         deal_words(1)
@@ -306,9 +313,10 @@ def tile_picked_expertpair_gelu_po_kernel(
         mul(1)
         sub(0)
         sub(1)
-        for c in range(2, NCH):
-            minus_b(c)
-            mul(c)
+        minus_b(2)
+        mul(2)
+        minus_b(3)
+        mul(3)
         for c in range(2, NCH):
             sub(c)
         half = S // 2

@@ -22,7 +22,7 @@ NCH = S // CH
 HALF = 256
 POOL_CHUNK = 1
 W2_SPLIT = 96
-W1_SPLIT = 92
+W1_SPLIT = 88
 
 
 def tile_picked_expertpair_gelu_po_kernel(
@@ -112,7 +112,7 @@ def tile_picked_expertpair_gelu_po_kernel(
         dealt = {}
 
         def deal_words(n):
-            ww[n] = keep.tile([P, N], U32, name="ww%d" % n, tag="w1_bf0" if n == 2 else "ww1", align_bytes=64)
+            ww[n] = keep.tile([P, N], U32, name="ww%d" % n, tag="w1_bf1" if n == 2 else "ww1", align_bytes=64)
             nc.vector.tensor_copy(
                 ww[n][:].rearrange("p (t g i) -> p g t i", t=PACK, i=4),
                 ww_raw[n][:].bitcast(U32).rearrange("p (g i t) -> p g t i", t=PACK, i=4),
@@ -182,7 +182,7 @@ def tile_picked_expertpair_gelu_po_kernel(
         nb_sb = {}
 
         def diff_b(c):
-            tags = (("bank22", "bank20"), ("bank23",), ("bank13",), ("bank22",))[c]
+            tags = (("bank22", "bank20"), ("bank23",), ("bank13",), ("bank20",))[c]
             diff[c] = [psum.tile([P, PACK // len(tags), CH], F32, name="diff%d%s" % (c, tag), tag=tag) for tag in tags]
             passes2(diff[c], 2, c, True, False, False)
 
@@ -281,7 +281,7 @@ def tile_picked_expertpair_gelu_po_kernel(
         quant_w1(1)
         for c in range(NCH):
             hid[1, c] = layer1(1, c)
-        nz["tile"] = keep.tile([P, NCH, CH * PACK], BF16, name="nz", tag="w1_bf1", align_bytes=64)
+        nz["tile"] = keep.tile([P, NCH, CH * PACK], BF16, name="nz", tag="w1_bf0", align_bytes=64)
         z1 = keep.tile([P, NCH, CH * PACK], BF16, name="z1", tag="z1", align_bytes=64)
         for c in range(2, NCH):
             gelu(2, c, hid[2, c], w_raw[1][:, 2 * c - 4 : 2 * c - 2, H - CH :].bitcast(BF16))
@@ -289,9 +289,9 @@ def tile_picked_expertpair_gelu_po_kernel(
         gelu(1, 1, hid[1, 1], z1[:, 0, :])
         gelu(1, 2, hid[1, 2], z1[:, 1, :])
         gelu(1, 3, hid[1, 3], z1[:, 2, :])
-        deal_words(2)
         negate(0)
         negate(1)
+        deal_words(2)
         quant_z(2, 0)
         quant_z(2, 1)
         deal_words(1)

@@ -20,9 +20,9 @@ PACK = 4
 CH = 128
 NCH = S // CH
 HALF = 256
+PAIR = 2
+W_SPLIT = 88
 POOL_CHUNK = 1
-W2_SPLIT = 96
-W1_SPLIT = 88
 
 
 def tile_picked_expertpair_gelu_po_kernel(
@@ -33,18 +33,20 @@ def tile_picked_expertpair_gelu_po_kernel(
         keep = ctx.enter_context(tc.tile_pool(name="keep", bufs=1))
         psum = ctx.enter_context(tc.psum_pool(name="psum", bufs=1))
 
+        def sb(shape, dtype, name, tag=None):
+            return keep.tile(shape, dtype, name=name, tag=tag or name, align_bytes=64)
+
         offs_t = keep.tile([P, S // 16], U16, name="offs_t")
         task_t = keep.tile([P, S // 16], U16, name="task_t")
-        xw = keep.tile([P, T], I32, name="xw", tag="xw", align_bytes=64)
-        xs = keep.tile([P, T], U8, name="xs", align_bytes=64)
-        ws_raw = keep.tile([P, N], U8, name="ws_raw", align_bytes=64)
-        ww_raw = {n: keep.tile([P, N], I32, name="ww_raw%d" % n, align_bytes=64) for n in (1, 2)}
-        mix_t = [keep.tile([P, U], F32, name="mix%d" % t, align_bytes=64) for t in range(PACK)]
-        w_raw = {n: keep.tile([P, PACK, H], F32, name="w_raw%d" % n, tag="w_raw%d" % n, align_bytes=64) for n in (1, 2)}
-        xg_w = [keep.tile([P, HALF], U32, name="xg_w%d" % h, align_bytes=64) for h in range(2)]
-        xg_rows = keep.tile([P, S], U8, name="xg_rows", align_bytes=64)
-        xg_s = keep.tile([P, S], U8, name="xg_s", align_bytes=64)
-        q4 = keep.tile([P, PACK, S], F32, name="q4", align_bytes=64)
+        xw = sb([P, T], I32, "xw")
+        xs = sb([P, T], U8, "xs")
+        ws_raw = sb([P, N], U8, "ws_raw")
+        ww_raw = {n: sb([P, N], I32, "ww_raw%d" % n) for n in (1, 2)}
+        mix_t = [sb([P, U], F32, "mix%d" % t) for t in range(PACK)]
+        w_raw = {n: sb([P, PACK, H], F32, "w_raw%d" % n) for n in (1, 2)}
+        xg_rows = sb([P, S], U8, "xg_rows")
+        xg_s = sb([P, S], U8, "xg_s")
+        q = [sb([P, PACK, CH], F32, "q%d" % c) for c in range(NCH)]
 
         nc.vector.memset(xs[:].bitcast(I32), 0)
         nc.vector.memset(ws_raw[:].bitcast(I32), 0)
@@ -59,47 +61,40 @@ def tile_picked_expertpair_gelu_po_kernel(
             nc.sync.dma_start(mix_t[t][:], mix_rows[:, t, :])
 
         def load_ws(n, quadrants):
-            for q in quadrants:
+            for r in quadrants:
                 nc.sync.dma_start(
-                    ws_raw[32 * q + 4 * n : 32 * q + 4 * n + 4, :].bitcast(I32), scales2[n][0, 4 * q : 4 * q + 4, :].bitcast(I32)
+                    ws_raw[32 * r + 4 * n : 32 * r + 4 * n + 4, :].bitcast(I32), scales2[n][0, 4 * r : 4 * r + 4, :].bitcast(I32)
                 )
 
         def load_ww(n):
             nc.sync.dma_start(ww_raw[n][:], words2[n][0].rearrange("p n t -> p (n t)").bitcast(I32))
 
-        def gather_q(t, halves=(0, 1)):
-            for h in halves:
-                nc.vector.tensor_copy(
-                    q4[:, t, h * HALF : (h + 1) * HALF], mix_t[t][:].indirect(task_t[:, h * 16 : (h + 1) * 16])
-                )
+        def gather_q(on_vector, c, planes):
+            for t in planes:
+                src = mix_t[t][:].indirect(task_t[:, c * 8 : (c + 1) * 8])
+                if on_vector:
+                    nc.vector.tensor_copy(q[c][:, t, :], src)
+                else:
+                    nc.scalar.activation(q[c][:, t, :], src, ACT.Copy)
 
-        w_bf = {2: keep.tile([P, PACK * H], BF16, name="w_bf2", align_bytes=64)}
-        w1_bf = [keep.tile([P, PACK * HALF], BF16, name="w1_bf%d" % h, tag="w1_bf%d" % h, align_bytes=64) for h in range(2)]
-        w_c = {n: keep.tile([P, H], U32, name="w_c%d" % n, align_bytes=64) for n in (1, 2)}
-        w_s = {n: keep.tile([P, H], U8, name="w_s%d" % n, align_bytes=64) for n in (1, 2)}
+        w2_bf = sb([P, PACK * H], BF16, "w2_bf")
+        w1_bf = [sb([P, PACK * HALF], BF16, "w1_bf%d" % h) for h in range(2)]
+        w_c = {n: sb([P, H], U32, "w_c%d" % n) for n in (1, 2)}
+        w_s = {n: sb([P, H], U8, "w_s%d" % n) for n in (1, 2)}
 
-        def cast_w(n, on_vector, ms):
-            dst = w_bf[n][:].rearrange("p (t m j) -> p m j t", t=PACK, j=PACK)[:, ms]
-            src = w_raw[n][:].rearrange("p j (m t) -> p m j t", t=PACK)[:, ms]
+        def round_w(on_vector, n, dst_tile, base, first, last):
+            dst = dst_tile[:].rearrange("p (t m j) -> p m j t", t=PACK, j=PACK)[:, first - base : last - base]
+            src = w_raw[n][:].rearrange("p j (m t) -> p m j t", t=PACK)[:, first:last]
             if on_vector:
                 nc.vector.tensor_copy(dst.rearrange("p m j t -> p m t j"), src.rearrange("p m j t -> p m t j"))
             else:
                 nc.scalar.copy(dst, src)
 
-        def quant_w(n, h):
+        def quant_w2(h):
             cols = slice(h * HALF, (h + 1) * HALF)
             nc.vector.quantize_mx(
-                out=w_c[n][:, cols].bitcast(FP8X4), scales=w_s[n][:, cols], in_=w_bf[n][:, h * HALF * PACK : (h + 1) * HALF * PACK]
+                out=w_c[2][:, cols].bitcast(FP8X4), scales=w_s[2][:, cols], in_=w2_bf[:, h * HALF * PACK : (h + 1) * HALF * PACK]
             )
-
-        def cast_w1(on_vector, first, last):
-            h = first // 64
-            dst = w1_bf[h][:].rearrange("p (t m j) -> p m j t", t=PACK, j=PACK)[:, first - 64 * h : last - 64 * h]
-            src = w_raw[1][:].rearrange("p j (m t) -> p m j t", t=PACK)[:, first:last]
-            if on_vector:
-                nc.vector.tensor_copy(dst.rearrange("p m j t -> p m t j"), src.rearrange("p m j t -> p m t j"))
-            else:
-                nc.scalar.copy(dst, src)
 
         def quant_w1(h):
             for t in range(PACK):
@@ -109,222 +104,245 @@ def tile_picked_expertpair_gelu_po_kernel(
                 )
 
         ww = {}
-        dealt = {}
 
-        def deal_words(n):
-            ww[n] = keep.tile([P, N], U32, name="ww%d" % n, tag="w1_bf1" if n == 2 else "ww1", align_bytes=64)
+        def deal_words(n, tag):
+            ww[n] = sb([P, N], U32, "ww%d" % n, tag)
             nc.vector.tensor_copy(
                 ww[n][:].rearrange("p (t g i) -> p g t i", t=PACK, i=4),
                 ww_raw[n][:].bitcast(U32).rearrange("p (g i t) -> p g t i", t=PACK, i=4),
             )
 
+        ws = sb([P, N], U8, "ws")
+
         def deal_scales():
-            ws = keep.tile([P, N], U8, name="ws", align_bytes=64)
-            dealt["ws"] = ws
             nc.vector.tensor_copy(ws[:].rearrange("p (t m) -> p t m", t=PACK), ws_raw[:].rearrange("p (m t) -> p t m", t=PACK))
 
-        z_bf = {}
-        z_c = {}
-        z_s = {}
+        xg = {}
 
-        def layer1(n, c):
-            cols = slice(c * CH, (c + 1) * CH)
-            gcols = slice(c % 2 * CH, (c % 2 + 1) * CH)
-            bank = psum.tile([P, PACK, CH], F32, name="hid%d%d" % (n, c), tag="bank%d%d" % (n, c % 2 if n == 2 else c))
+        def gather_x(first, count, tag=None):
+            tile = sb([P, count * CH], U32, "xg%d" % first, tag)
+            nc.vector.tensor_copy(tile[:], xw[:].bitcast(U32).indirect(offs_t[:, first * 8 : (first + count) * 8]))
+            for c in range(count):
+                xg[first + c] = tile[:, c * CH : (c + 1) * CH]
+
+        hid = {}
+
+        def layer1(n, c, bank):
+            hid[n, c] = psum.tile([P, PACK, CH], F32, name="hid%d%d" % (n, c), tag=bank)
             for t in range(PACK):
-                tc_ = slice(t * P, (t + 1) * P)
+                cols = slice(t * P, (t + 1) * P)
                 nc.tensor.matmul_mx(
-                    out=bank[:, t, :],
-                    lhsT=w_c[n][:, tc_].bitcast(FP8X4),
-                    lhsT_scale=w_s[n][:, tc_],
-                    rhs=xg_w[c // 2][:, gcols].bitcast(FP8X4),
-                    rhs_scale=xg_s[:, cols],
+                    out=hid[n, c][:, t, :],
+                    lhsT=w_c[n][:, cols].bitcast(FP8X4),
+                    lhsT_scale=w_s[n][:, cols],
+                    rhs=xg[c].bitcast(FP8X4),
+                    rhs_scale=xg_s[:, c * CH : (c + 1) * CH],
                     start=True,
                     stop=True,
                 )
-            return bank
 
-        def gelu(n, c, bank, dst):
+        z_bf = {}
+
+        def gelu(n, c, dst):
             z_bf[n, c] = dst
-            if len(dst.shape) == 3:
-                nc.scalar.activation(dst.rearrange("p a (s t) -> p a s t", t=PACK), bank[:].rearrange("p t (a s) -> p a s t", a=2), ACT.Gelu_apprx_tanh)
-            else:
-                nc.scalar.activation(dst.rearrange("p (s t) -> p s t", t=PACK), bank[:].rearrange("p t s -> p s t"), ACT.Gelu_apprx_tanh)
+            nc.scalar.activation(
+                dst.rearrange("p a (s t) -> p a s t", t=PACK), hid[n, c][:].rearrange("p t (a s) -> p a s t", a=2), ACT.Gelu_apprx_tanh
+            )
+
+        def gelu1(c):
+            gelu(1, c, q[c + 1][:, PAIR:, :].bitcast(BF16) if c in (1, 2) else sb([P, 2, HALF], BF16, "z1_%d" % c)[:])
 
         nz = {}
 
-        def negate(c):
-            nz[c] = nz["tile"][:, c, :]
-            nc.vector.tensor_scalar_mul(nz[c].rearrange("p (a x) -> p a x", a=2) if c > 1 else nz[c], z_bf[2, c], -1.0)
+        def negate(c, dst):
+            nz[c] = dst
+            nc.vector.tensor_scalar_mul(dst, z_bf[2, c], -1.0)
 
-        def quant_z(n, c):
-            z_c[n, c] = keep.tile([P, CH], U32, name="z_c%d%d" % (n, c), align_bytes=64)
-            z_s[n, c] = keep.tile([P, CH], U8, name="z_s%d%d" % (n, c), align_bytes=64)
+        z_c = {}
+        z_s = {}
+
+        def quant_z(n, c, tag=None):
+            z_c[n, c] = sb([P, CH], U32, "z_c%d%d" % (n, c), tag)[:]
+            z_s[n, c] = sb([P, CH], U8, "z_s%d%d" % (n, c))[:]
             src = nz[c] if n == 2 else z_bf[1, c]
-            nc.vector.quantize_mx(out=z_c[n, c][:].bitcast(FP8X4), scales=z_s[n, c][:], in_=src)
+            nc.vector.quantize_mx(out=z_c[n, c].bitcast(FP8X4), scales=z_s[n, c], in_=src.rearrange("p a x -> p (a x)"))
+
+        def quant_pair(first, src, tag):
+            codes = sb([P, 2 * CH], U32, "z_pair_c%d" % first, tag)
+            scales = sb([P, 2 * CH], U8, "z_pair_s%d" % first)
+            nc.vector.quantize_mx(out=codes[:].bitcast(FP8X4), scales=scales[:], in_=src[:].rearrange("p c a x -> p (c a x)"))
+            for i in range(2):
+                z_c[2, first + i] = codes[:, i * CH : (i + 1) * CH]
+                z_s[2, first + i] = scales[:, i * CH : (i + 1) * CH]
 
         def passes2(banks, n, c, opens, closes, lone):
             per = PACK // len(banks)
             for t in range(PACK):
-                tc_ = slice(t * P, (t + 1) * P)
+                cols = slice(t * P, (t + 1) * P)
                 nc.tensor.matmul_mx(
                     out=banks[t // per][:, t % per, :],
-                    lhsT=ww[n][:, tc_].bitcast(FP8X4),
-                    lhsT_scale=dealt["ws"][4 * n : P, tc_],
-                    rhs=z_c[n, c][:].bitcast(FP8X4),
-                    rhs_scale=z_s[n, c][:],
+                    lhsT=ww[n][:, cols].bitcast(FP8X4),
+                    lhsT_scale=ws[4 * n : P, cols],
+                    rhs=z_c[n, c].bitcast(FP8X4),
+                    rhs_scale=z_s[n, c],
                     start=lone or (opens and t % per == 0),
                     stop=lone or (closes and t % per == per - 1),
                 )
 
-        nb = {}
         diff = {}
-        nb_sb = {}
+        nb = {}
 
-        def diff_b(c):
-            tags = (("bank22", "bank20"), ("bank23",), ("bank13",), ("bank20",))[c]
-            diff[c] = [psum.tile([P, PACK // len(tags), CH], F32, name="diff%d%s" % (c, tag), tag=tag) for tag in tags]
+        def diff_b(c, banks):
+            diff[c] = [psum.tile([P, PACK // len(banks), CH], F32, name="diff%d%s" % (c, b), tag=b) for b in banks]
             passes2(diff[c], 2, c, True, False, False)
 
         def diff_a(c):
             passes2(diff[c], 1, c, False, True, False)
 
-        def minus_b(c):
-            nb[c] = psum.tile([P, PACK, CH], F32, name="nb%d" % c, tag=("bank12", "bank11", "bank12", "bank13")[c])
+        def minus_b(c, bank):
+            nb[c] = psum.tile([P, PACK, CH], F32, name="nb%d" % c, tag=bank)
             passes2([nb[c]], 2, c, False, False, True)
-            if c == POOL_CHUNK:
-                nb_sb[c] = keep.tile([P, PACK, CH], F32, name="nb_sb%d" % c, align_bytes=64)
-                nc.scalar.copy(nb_sb[c][:], nb[c][:])
 
-        o_c = keep.tile([P, S], I32, name="o_c", align_bytes=64)
-        o_s = keep.tile([P, S], U8, name="o_s", align_bytes=64)
+        o_c = sb([P, S], I32, "o_c")
+        o_s = sb([P, S], U8, "o_s")
         out_rows = out_0.rearrange("(p t) s -> p t s", t=PACK)
         o1 = out_1[0].rearrange("p n t -> p (n t)").bitcast(I32)
         prod = {}
         y = {}
-        y_bf = {}
+        y_bf = [sb([P, 2 * CH * PACK], BF16, "y_bf%d" % h) for h in range(2)]
 
         def mul(c):
-            cols = slice(c * CH, (c + 1) * CH)
-            prod[c] = keep.tile([P, PACK, CH], F32, name="prod%d" % c, tag="prod%d" % c, align_bytes=64)
+            prod[c] = sb([P, PACK, CH], F32, "prod%d" % c)
             per = PACK // len(diff[c])
             for i, bank in enumerate(diff[c]):
                 ts = slice(i * per, (i + 1) * per)
-                nc.vector.tensor_tensor(prod[c][:, ts, :], bank[:], q4[:, ts, cols], ALU.mult)
+                nc.vector.tensor_tensor(prod[c][:, ts, :], bank[:], q[c][:, ts, :], ALU.mult)
 
         def sub(c):
-            cols = slice(c * CH, (c + 1) * CH)
-            y[c] = keep.tile([P, PACK, CH], F32, name="y%d" % c, tag="z1" if c == POOL_CHUNK else "y%d" % c, align_bytes=64)
+            y[c] = sb([P, PACK, CH], F32, "y%d" % c, "z1_3" if c == POOL_CHUNK else None)
             if c == POOL_CHUNK:
-                nc.gpsimd.tensor_tensor(y[c][:], prod[c][:], nb_sb[c][:], ALU.subtract)
+                nc.gpsimd.tensor_tensor(y[c][:], prod[c][:], nb_sb, ALU.subtract)
             else:
                 nc.vector.tensor_tensor(y[c][:], prod[c][:], nb[c][:], ALU.subtract)
-            nc.sync.dma_start(out_rows[:, :, cols], y[c][:])
-            if c % 2 == 0:
-                y_bf[c // 2] = keep.tile([P, 2 * CH * PACK], BF16, name="y_bf%d" % c, tag="prod0" if c == 0 else "y_bf", align_bytes=64)
+            nc.sync.dma_start(out_rows[:, :, c * CH : (c + 1) * CH], y[c][:])
+
+        def round_y(on_vector, c, first, last):
             dst = y_bf[c // 2][:, c % 2 * CH * PACK : (c % 2 + 1) * CH * PACK].rearrange("p (g i t) -> p g t i", i=4, t=PACK)
             src = y[c][:].rearrange("p t (g i) -> p g t i", i=4)
-            if c < NCH - 1:
-                nc.scalar.copy(dst, src)
+            if on_vector:
+                nc.vector.tensor_copy(dst[:, first:last], src[:, first:last])
             else:
-                nc.scalar.copy(dst[:, :16], src[:, :16])
-                nc.vector.tensor_copy(dst[:, 16:], src[:, 16:])
+                nc.scalar.copy(dst[:, first:last], src[:, first:last])
 
         def quant_y(first, last):
             cols = slice(first * CH, last * CH)
+            base = first // 2 * 2
             nc.vector.quantize_mx(
-                out=o_c[:, cols].bitcast(FP8X4), scales=o_s[:, cols], in_=y_bf[first // 2][:, first % 2 * CH * PACK : (last - first // 2 * 2) * CH * PACK]
+                out=o_c[:, cols].bitcast(FP8X4), scales=o_s[:, cols], in_=y_bf[first // 2][:, (first - base) * CH * PACK : (last - base) * CH * PACK]
             )
 
         load_mix(0)
         nc.sync.dma_start(task_t[:], task)
-        load_mix(1)
         nc.sync.dma_start(offs_t[:], offs)
         nc.sync.dma_start(xs[0:P:8, :].bitcast(I32), x_scales[0].bitcast(I32))
         load_ws(2, (0, 1))
         nc.sync.dma_start(w_raw[2][:], w_rows[2])
-        load_mix(2)
         load_ws(2, (2, 3))
-        load_ws(1, (0, 1, 2))
+        load_ws(1, range(4))
         nc.sync.dma_start(xw[:], x_words[0].rearrange("p n t -> p (n t)").bitcast(I32))
 
-        gather_q(0)
-        gather_q(1)
+        for c in range(NCH):
+            gather_q(True, c, (0,))
         nc.vector.tensor_copy(xg_rows[:], xs[:].indirect(offs_t[:]))
-        load_mix(3)
-        load_ws(1, (3,))
         for r in range(4):
             nc.sync.dma_start(xg_s[r:P:32, :].bitcast(I32), xg_rows[8 * r : P : 32, :].bitcast(I32))
-        nc.sync.dma_start(w_raw[1][:], w_rows[1])
+        load_mix(1)
         load_ww(2)
+        nc.sync.dma_start(w_raw[1][:], w_rows[1])
+        load_mix(2)
         load_ww(1)
-        cast_w(2, False, slice(0, W2_SPLIT))
-        cast_w(2, True, slice(W2_SPLIT, P))
-        gather_q(2)
-        quant_w(2, 0)
-        quant_w(2, 1)
-        for h in range(2):
-            nc.vector.tensor_copy(xg_w[h][:], xw[:].bitcast(U32).indirect(offs_t[:, h * 16 : (h + 1) * 16]))
-        gather_q(3)
+        load_mix(3)
+
+        round_w(False, 2, w2_bf, 0, W_SPLIT, P)
+        round_w(True, 2, w2_bf, 0, 0, W_SPLIT)
+        quant_w2(0)
+        quant_w2(1)
+        gather_x(0, 1)
+        gather_x(1, 1)
+        gather_x(2, 2)
         deal_scales()
-        hid = {(2, c): layer1(2, c) for c in range(2)}
-        z20 = keep.tile([P, CH * PACK], BF16, name="z20", align_bytes=64)
-        z21 = keep.tile([P, CH * PACK], BF16, name="z21", align_bytes=64)
-        gelu(2, 0, hid[2, 0], z20[:])
-        gelu(2, 1, hid[2, 1], z21[:])
-        for c in range(2, NCH):
-            hid[2, c] = layer1(2, c)
-        cast_w1(False, W1_SPLIT, P)
-        cast_w1(True, 0, 64)
-        cast_w1(True, 64, W1_SPLIT)
+        for c in range(NCH):
+            gather_q(True, c, (1,))
+        deal_words(2, None)
+        for c in range(NCH):
+            layer1(2, c, "ABCD"[c])
+            gelu(2, c, sb([P, 2, HALF], BF16, "z2_%d" % c)[:])
+        nz01 = sb([P, 2, 2, HALF], BF16, "nz01")
+        negate(0, nz01[:, 0])
+        negate(1, nz01[:, 1])
+        quant_pair(0, nz01, None)
+        diff_b(0, "EF")
+        minus_b(1, "G")
+        minus_b(0, "H")
+
+        round_w(False, 1, w1_bf[1], 64, W_SPLIT, P)
+        round_w(True, 1, w1_bf[0], 0, 0, 64)
+        round_w(True, 1, w1_bf[1], 64, 64, W_SPLIT)
         quant_w1(0)
         quant_w1(1)
-        for c in range(NCH):
-            hid[1, c] = layer1(1, c)
-        nz["tile"] = keep.tile([P, NCH, CH * PACK], BF16, name="nz", tag="w1_bf0", align_bytes=64)
-        z1 = keep.tile([P, NCH, CH * PACK], BF16, name="z1", tag="z1", align_bytes=64)
-        for c in range(2, NCH):
-            gelu(2, c, hid[2, c], w_raw[1][:, 2 * c - 4 : 2 * c - 2, H - CH :].bitcast(BF16))
-        gelu(1, 0, hid[1, 0], z1[:, 3, :])
-        gelu(1, 1, hid[1, 1], z1[:, 0, :])
-        gelu(1, 2, hid[1, 2], z1[:, 1, :])
-        gelu(1, 3, hid[1, 3], z1[:, 2, :])
-        negate(0)
-        negate(1)
-        deal_words(2)
-        quant_z(2, 0)
-        quant_z(2, 1)
-        deal_words(1)
-        for c in range(2):
-            diff_b(c)
-            quant_z(1, c)
-            diff_a(c)
-        minus_b(1)
-        minus_b(0)
-        for c in range(2, NCH):
-            negate(c)
-        for c in range(2, NCH):
-            quant_z(2, c)
+        layer1(1, 0, "A")
+        layer1(1, 1, "B")
+        layer1(1, 2, "C")
+        nb_sb = w_raw[1][:, :, H - CH :]
+        gather_q(False, 0, (2,))
+        nc.scalar.copy(nb_sb, nb[1][:])
+        gather_q(False, 1, (2,))
+        deal_words(1, "w1_bf1")
+        gelu1(0)
+        quant_z(1, 0)
+        diff_a(0)
+        layer1(1, 3, "D")
+        diff_b(1, "G")
+        nz23 = sb([P, 2, 2, HALF], BF16, "nz23", "w1_bf0")
+        negate(2, nz23[:, 0])
+        negate(3, nz23[:, 1])
+        gather_q(True, 0, (3,))
+        quant_pair(2, nz23, None)
+        gather_q(True, 1, (3,))
+        gelu1(1)
+        quant_z(1, 1)
+        diff_a(1)
+        gelu1(2)
+        gelu1(3)
+        gather_q(False, 2, (2, 3))
+
         mul(0)
-        for c in range(2, NCH):
-            quant_z(1, c)
-            diff_b(c)
-            diff_a(c)
+        quant_z(1, 2)
+        gather_q(False, 3, (2, 3))
+        diff_b(2, "B")
+        diff_a(2)
         mul(1)
+        quant_z(1, 3)
+        diff_b(3, "D")
+        diff_a(3)
         sub(0)
+        minus_b(2, "H")
+        minus_b(3, "G")
         sub(1)
-        minus_b(2)
+        round_y(False, 0, 0, 32)
+        round_y(False, 1, 0, 32)
         mul(2)
-        minus_b(3)
         mul(3)
-        for c in range(2, NCH):
-            sub(c)
-        half = S // 2
+        sub(2)
+        round_y(False, 2, 0, 32)
+        sub(3)
         quant_y(0, 2)
-        nc.sync.dma_start(o1[:, :half], o_c[:, :half])
+        nc.sync.dma_start(o1[:, :HALF], o_c[:, :HALF])
+        round_y(False, 3, 0, 16)
+        round_y(True, 3, 16, 32)
         quant_y(2, 3)
         quant_y(3, 4)
-        nc.sync.dma_start(o1[:, half:], o_c[:, half:])
-        for q in range(4):
-            eng = nc.scalar if q % 2 else nc.sync
-            eng.dma_start(out_2[0, 4 * q : 4 * q + 4, :].bitcast(I32), o_s[32 * q : 32 * q + 4, :].bitcast(I32))
+        nc.sync.dma_start(o1[:, HALF:], o_c[:, HALF:])
+        for r in range(4):
+            eng = nc.scalar if r % 2 else nc.sync
+            eng.dma_start(out_2[0, 4 * r : 4 * r + 4, :].bitcast(I32), o_s[32 * r : 32 * r + 4, :].bitcast(I32))

@@ -22,6 +22,7 @@ NCH = S // CH
 HALF = 256
 PAIR = 2
 W_SPLIT = 88
+W2_SPLIT = 48
 POOL_CHUNK = 1
 
 
@@ -46,7 +47,8 @@ def tile_picked_expertpair_gelu_po_kernel(
         w_raw = {n: sb([P, PACK, H], F32, "w_raw%d" % n) for n in (1, 2)}
         xg_rows = sb([P, S], U8, "xg_rows")
         xg_s = sb([P, S], U8, "xg_s")
-        q = [sb([P, PACK, CH], F32, "q%d" % c) for c in range(NCH)]
+        q_flat = sb([P, PACK * S + CH], F32, "q_flat")
+        q = q_flat[:, : PACK * S].rearrange("p (t s) -> p t s", t=PACK)
 
         nc.vector.memset(xs[:].bitcast(I32), 0)
         nc.vector.memset(ws_raw[:].bitcast(I32), 0)
@@ -69,13 +71,17 @@ def tile_picked_expertpair_gelu_po_kernel(
         def load_ww(n):
             nc.sync.dma_start(ww_raw[n][:], words2[n][0].rearrange("p n t -> p (n t)").bitcast(I32))
 
-        def gather_q(on_vector, c, planes):
-            for t in planes:
-                src = mix_t[t][:].indirect(task_t[:, c * 8 : (c + 1) * 8])
-                if on_vector:
-                    nc.vector.tensor_copy(q[c][:, t, :], src)
-                else:
-                    nc.scalar.activation(q[c][:, t, :], src, ACT.Copy)
+        def gather_q(on_vector, t, first, count):
+            src = mix_t[t][:].indirect(task_t[:, first * 8 : (first + count) * 8])
+            dst = q[:, t, first * CH : (first + count) * CH]
+            if on_vector:
+                nc.vector.tensor_copy(dst, src)
+            else:
+                nc.scalar.activation(dst, src, ACT.Copy)
+
+        def gather_plane(t):
+            for h in range(2):
+                gather_q(True, t, 2 * h, 2)
 
         w2_bf = sb([P, PACK * H], BF16, "w2_bf")
         w1_bf = [sb([P, PACK * HALF], BF16, "w1_bf%d" % h) for h in range(2)]
@@ -150,7 +156,9 @@ def tile_picked_expertpair_gelu_po_kernel(
             )
 
         def gelu1(c):
-            gelu(1, c, q[c + 1][:, PAIR:, :].bitcast(BF16) if c in (1, 2) else sb([P, 2, HALF], BF16, "z1_%d" % c)[:])
+            first = (PACK - 1) * S + CH + c % 2 * HALF
+            late = q_flat[:, first : first + HALF].bitcast(BF16).rearrange("p (a x) -> p a x", a=2)
+            gelu(1, c, late if c < 2 else sb([P, 2, HALF], BF16, "z1_%d" % c)[:])
 
         nz = {}
 
@@ -170,7 +178,7 @@ def tile_picked_expertpair_gelu_po_kernel(
         def quant_pair(first, src, tag):
             codes = sb([P, 2 * CH], U32, "z_pair_c%d" % first, tag)
             scales = sb([P, 2 * CH], U8, "z_pair_s%d" % first)
-            nc.vector.quantize_mx(out=codes[:].bitcast(FP8X4), scales=scales[:], in_=src[:].rearrange("p c a x -> p (c a x)"))
+            nc.vector.quantize_mx(out=codes[:].bitcast(FP8X4), scales=scales[:], in_=src.rearrange("p c a x -> p (c a x)"))
             for i in range(2):
                 z_c[2, first + i] = codes[:, i * CH : (i + 1) * CH]
                 z_s[2, first + i] = scales[:, i * CH : (i + 1) * CH]
@@ -216,7 +224,7 @@ def tile_picked_expertpair_gelu_po_kernel(
             per = PACK // len(diff[c])
             for i, bank in enumerate(diff[c]):
                 ts = slice(i * per, (i + 1) * per)
-                nc.vector.tensor_tensor(prod[c][:, ts, :], bank[:], q[c][:, ts, :], ALU.mult)
+                nc.vector.tensor_tensor(prod[c][:, ts, :], bank[:], q[:, ts, c * CH : (c + 1) * CH], ALU.mult)
 
         def sub(c):
             y[c] = sb([P, PACK, CH], F32, "y%d" % c, "z1_3" if c == POOL_CHUNK else None)
@@ -245,93 +253,92 @@ def tile_picked_expertpair_gelu_po_kernel(
         nc.sync.dma_start(task_t[:], task)
         nc.sync.dma_start(offs_t[:], offs)
         nc.sync.dma_start(xs[0:P:8, :].bitcast(I32), x_scales[0].bitcast(I32))
+        load_mix(1)
         load_ws(2, (0, 1))
         nc.sync.dma_start(w_raw[2][:], w_rows[2])
         load_ws(2, (2, 3))
-        load_ws(1, range(4))
+        load_ws(1, range(3))
         nc.sync.dma_start(xw[:], x_words[0].rearrange("p n t -> p (n t)").bitcast(I32))
 
-        for c in range(NCH):
-            gather_q(True, c, (0,))
+        gather_plane(0)
+        gather_plane(1)
         nc.vector.tensor_copy(xg_rows[:], xs[:].indirect(offs_t[:]))
+        load_ws(1, (3,))
         for r in range(4):
             nc.sync.dma_start(xg_s[r:P:32, :].bitcast(I32), xg_rows[8 * r : P : 32, :].bitcast(I32))
-        load_mix(1)
-        load_ww(2)
-        nc.sync.dma_start(w_raw[1][:], w_rows[1])
         load_mix(2)
-        load_ww(1)
+        nc.sync.dma_start(w_raw[1][:], w_rows[1])
         load_mix(3)
+        load_ww(2)
+        load_ww(1)
 
-        round_w(False, 2, w2_bf, 0, W_SPLIT, P)
-        round_w(True, 2, w2_bf, 0, 0, W_SPLIT)
+        round_w(False, 2, w2_bf, 0, W2_SPLIT, P)
+        round_w(True, 2, w2_bf, 0, 0, W2_SPLIT)
         quant_w2(0)
         quant_w2(1)
         gather_x(0, 1)
         gather_x(1, 1)
         gather_x(2, 2)
+        gather_plane(2)
         deal_scales()
-        for c in range(NCH):
-            gather_q(True, c, (1,))
-        deal_words(2, None)
-        for c in range(NCH):
-            layer1(2, c, "ABCD"[c])
+        for c in range(2):
+            layer1(2, c, "AB"[c])
             gelu(2, c, sb([P, 2, HALF], BF16, "z2_%d" % c)[:])
-        nz01 = sb([P, 2, 2, HALF], BF16, "nz01")
-        negate(0, nz01[:, 0])
-        negate(1, nz01[:, 1])
-        quant_pair(0, nz01, None)
-        diff_b(0, "EF")
-        minus_b(1, "G")
-        minus_b(0, "H")
+        for c in range(2, NCH):
+            layer1(2, c, "AB"[c % 2])
 
         round_w(False, 1, w1_bf[1], 64, W_SPLIT, P)
         round_w(True, 1, w1_bf[0], 0, 0, 64)
         round_w(True, 1, w1_bf[1], 64, 64, W_SPLIT)
         quant_w1(0)
         quant_w1(1)
-        layer1(1, 0, "A")
-        layer1(1, 1, "B")
-        layer1(1, 2, "C")
-        nb_sb = w_raw[1][:, :, H - CH :]
-        gather_q(False, 0, (2,))
-        nc.scalar.copy(nb_sb, nb[1][:])
-        gather_q(False, 1, (2,))
-        deal_words(1, "w1_bf1")
+        for c in range(NCH):
+            layer1(1, c, "CDEF"[c])
+        gather_q(False, 3, 0, 1)
+        for c in range(2, NCH):
+            gelu(2, c, w_raw[1][:, 2 * c - 4 : 2 * c - 2, H - CH :].bitcast(BF16))
+        nz_all = sb([P, NCH, 2, HALF], BF16, "nz_all", "w1_bf0")
+        negate(0, nz_all[:, 0])
+        negate(1, nz_all[:, 1])
+        deal_words(2, "w1_bf1")
+        quant_pair(0, nz_all[:, :2], None)
+        deal_words(1, None)
+        diff_b(0, "GA")
         gelu1(0)
         quant_z(1, 0)
         diff_a(0)
-        layer1(1, 3, "D")
-        diff_b(1, "G")
-        nz23 = sb([P, 2, 2, HALF], BF16, "nz23", "w1_bf0")
-        negate(2, nz23[:, 0])
-        negate(3, nz23[:, 1])
-        gather_q(True, 0, (3,))
-        quant_pair(2, nz23, None)
-        gather_q(True, 1, (3,))
+        diff_b(1, "H")
         gelu1(1)
         quant_z(1, 1)
         diff_a(1)
+        minus_b(1, "D")
+        minus_b(0, "E")
+        negate(2, nz_all[:, 2])
+        negate(3, nz_all[:, 3])
+        quant_pair(2, nz_all[:, 2:], None)
         gelu1(2)
+        gather_q(False, 3, 1, 1)
         gelu1(3)
-        gather_q(False, 2, (2, 3))
+        nb_sb = sb([P, PACK, CH], F32, "nb_sb")[:]
+        nc.scalar.copy(nb_sb, nb[1][:])
+        gather_q(False, 3, 2, 1)
 
         mul(0)
         quant_z(1, 2)
-        gather_q(False, 3, (2, 3))
-        diff_b(2, "B")
+        gather_q(False, 3, 3, 1)
+        diff_b(2, "F")
         diff_a(2)
         mul(1)
         quant_z(1, 3)
-        diff_b(3, "D")
+        diff_b(3, "A")
         diff_a(3)
         sub(0)
-        minus_b(2, "H")
-        minus_b(3, "G")
         sub(1)
         round_y(False, 0, 0, 32)
         round_y(False, 1, 0, 32)
+        minus_b(2, "E")
         mul(2)
+        minus_b(3, "F")
         mul(3)
         sub(2)
         round_y(False, 2, 0, 32)

@@ -22,7 +22,7 @@ NCH = S // CH
 HALF = 256
 PAIR = 2
 W_SPLIT = 88
-W2_SPLIT = 48
+W2_SPLIT = 96
 POOL_CHUNK = 1
 
 
@@ -79,9 +79,9 @@ def tile_picked_expertpair_gelu_po_kernel(
             else:
                 nc.scalar.activation(dst, src, ACT.Copy)
 
-        def gather_plane(t):
+        def gather_plane(on_vector, t):
             for h in range(2):
-                gather_q(True, t, 2 * h, 2)
+                gather_q(on_vector, t, 2 * h, 2)
 
         w2_bf = sb([P, PACK * H], BF16, "w2_bf")
         w1_bf = [sb([P, PACK * HALF], BF16, "w1_bf%d" % h) for h in range(2)]
@@ -251,19 +251,18 @@ def tile_picked_expertpair_gelu_po_kernel(
 
         load_mix(0)
         nc.sync.dma_start(task_t[:], task)
+        load_mix(1)
         nc.sync.dma_start(offs_t[:], offs)
         nc.sync.dma_start(xs[0:P:8, :].bitcast(I32), x_scales[0].bitcast(I32))
-        load_mix(1)
         load_ws(2, (0, 1))
         nc.sync.dma_start(w_raw[2][:], w_rows[2])
         load_ws(2, (2, 3))
-        load_ws(1, range(3))
+        load_ws(1, range(4))
         nc.sync.dma_start(xw[:], x_words[0].rearrange("p n t -> p (n t)").bitcast(I32))
 
-        gather_plane(0)
-        gather_plane(1)
+        gather_plane(True, 0)
+        gather_plane(False, 1)
         nc.vector.tensor_copy(xg_rows[:], xs[:].indirect(offs_t[:]))
-        load_ws(1, (3,))
         for r in range(4):
             nc.sync.dma_start(xg_s[r:P:32, :].bitcast(I32), xg_rows[8 * r : P : 32, :].bitcast(I32))
         load_mix(2)
@@ -276,16 +275,17 @@ def tile_picked_expertpair_gelu_po_kernel(
         round_w(True, 2, w2_bf, 0, 0, W2_SPLIT)
         quant_w2(0)
         quant_w2(1)
+        deal_scales()
         gather_x(0, 1)
         gather_x(1, 1)
         gather_x(2, 2)
-        gather_plane(2)
-        deal_scales()
+        gather_plane(True, 2)
         for c in range(2):
             layer1(2, c, "AB"[c])
             gelu(2, c, sb([P, 2, HALF], BF16, "z2_%d" % c)[:])
-        for c in range(2, NCH):
-            layer1(2, c, "AB"[c % 2])
+        negate(0, sb([P, 2, HALF], BF16, "nz0")[:])
+        layer1(2, 2, "A")
+        layer1(2, 3, "B")
 
         round_w(False, 1, w1_bf[1], 64, W_SPLIT, P)
         round_w(True, 1, w1_bf[0], 0, 0, 64)
@@ -298,10 +298,10 @@ def tile_picked_expertpair_gelu_po_kernel(
         for c in range(2, NCH):
             gelu(2, c, w_raw[1][:, 2 * c - 4 : 2 * c - 2, H - CH :].bitcast(BF16))
         nz_all = sb([P, NCH, 2, HALF], BF16, "nz_all", "w1_bf0")
-        negate(0, nz_all[:, 0])
         negate(1, nz_all[:, 1])
-        deal_words(2, "w1_bf1")
-        quant_pair(0, nz_all[:, :2], None)
+        quant_z(2, 0, "w1_bf1")
+        deal_words(2, None)
+        quant_z(2, 1)
         deal_words(1, None)
         diff_b(0, "GA")
         gelu1(0)

from contextlib import ExitStack

import concourse.mybir as mybir

K, T, S, N, H, U = 512, 2048, 512, 512, 512, 512
FLOPS = 4 * 2 * 512 * 512 * 512

F32 = mybir.dt.float32
BF16 = mybir.dt.bfloat16
I32 = mybir.dt.int32
U32 = mybir.dt.uint32
U16 = mybir.dt.uint16
U8 = mybir.dt.uint8
FP8X4 = mybir.dt.float8_e4m3fn_x4
ALU = mybir.AluOpType
ACT = mybir.ActivationFunctionType

P = 128
PACK = 4
CH = 128
NCH = S // CH
HALF = 256
PAIR = 2
W_SPLIT = 88
W2_SPLIT = 96
POOL_CHUNK = 1


def tile_picked_expertpair_gelu_po_kernel(
    tc, x_words, x_scales, w1, w2, w3_words, w3_scales, w4_words, w4_scales, mix, offs, task, out_0, out_1, out_2
):
    nc = tc.nc
    with ExitStack() as ctx:
        keep = ctx.enter_context(tc.tile_pool(name="keep", bufs=1))
        psum = ctx.enter_context(tc.psum_pool(name="psum", bufs=1))

        def sb(shape, dtype, name, tag=None):
            return keep.tile(shape, dtype, name=name, tag=tag or name, align_bytes=64)

        offs_t = keep.tile([P, S // 16], U16, name="offs_t")
        task_t = keep.tile([P, S // 16], U16, name="task_t")
        xw = sb([P, T], I32, "xw")
        xs = sb([P, T], U8, "xs")
        ws_raw = sb([P, N], U8, "ws_raw")
        ww_raw = {n: sb([P, N], I32, "ww_raw%d" % n) for n in (1, 2)}
        mix_t = [sb([P, U], F32, "mix%d" % t) for t in range(PACK)]
        w_raw = {n: sb([P, PACK, H], F32, "w_raw%d" % n) for n in (1, 2)}
        xg_rows = sb([P, S], U8, "xg_rows")
        xg_s = sb([P, S], U8, "xg_s")
        q_flat = sb([P, PACK * S + CH], F32, "q_flat")
        q = q_flat[:, : PACK * S].rearrange("p (t s) -> p t s", t=PACK)

        nc.vector.memset(xs[:].bitcast(I32), 0)
        nc.vector.memset(ws_raw[:].bitcast(I32), 0)
        nc.vector.memset(xg_s[:].bitcast(I32), 0)

        mix_rows = mix.rearrange("(p t) u -> p t u", t=PACK)
        w_rows = {1: w1.rearrange("(p j) c -> p j c", j=PACK), 2: w2.rearrange("(p j) c -> p j c", j=PACK)}
        words2 = {1: w3_words, 2: w4_words}
        scales2 = {1: w3_scales, 2: w4_scales}

        def load_mix(t):
            nc.sync.dma_start(mix_t[t][:], mix_rows[:, t, :])

        def load_ws(n, quadrants):
            for r in quadrants:
                nc.sync.dma_start(
                    ws_raw[32 * r + 4 * n : 32 * r + 4 * n + 4, :].bitcast(I32), scales2[n][0, 4 * r : 4 * r + 4, :].bitcast(I32)
                )

        def load_ww(n):
            nc.sync.dma_start(ww_raw[n][:], words2[n][0].rearrange("p n t -> p (n t)").bitcast(I32))

        def gather_q(on_vector, t, first, count):
            src = mix_t[t][:].indirect(task_t[:, first * 8 : (first + count) * 8])
            dst = q[:, t, first * CH : (first + count) * CH]
            if on_vector:
                nc.vector.tensor_copy(dst, src)
            else:
                nc.scalar.activation(dst, src, ACT.Copy)

        def gather_plane(on_vector, t):
            for h in range(2):
                gather_q(on_vector, t, 2 * h, 2)

        w2_bf = sb([P, PACK * H], BF16, "w2_bf")
        w1_bf = [sb([P, PACK * HALF], BF16, "w1_bf%d" % h) for h in range(2)]
        w_c = {n: sb([P, H], U32, "w_c%d" % n) for n in (1, 2)}
        w_s = {n: sb([P, H], U8, "w_s%d" % n) for n in (1, 2)}

        def round_w(on_vector, n, dst_tile, base, first, last):
            dst = dst_tile[:].rearrange("p (t m j) -> p m j t", t=PACK, j=PACK)[:, first - base : last - base]
            src = w_raw[n][:].rearrange("p j (m t) -> p m j t", t=PACK)[:, first:last]
            if on_vector:
                nc.vector.tensor_copy(dst.rearrange("p m j t -> p m t j"), src.rearrange("p m j t -> p m t j"))
            else:
                nc.scalar.copy(dst, src)

        def quant_w2(h):
            cols = slice(h * HALF, (h + 1) * HALF)
            nc.vector.quantize_mx(
                out=w_c[2][:, cols].bitcast(FP8X4), scales=w_s[2][:, cols], in_=w2_bf[:, h * HALF * PACK : (h + 1) * HALF * PACK]
            )

        def quant_w1(h):
            for t in range(PACK):
                cols = slice(t * P + h * 64, t * P + (h + 1) * 64)
                nc.vector.quantize_mx(
                    out=w_c[1][:, cols].bitcast(FP8X4), scales=w_s[1][:, cols], in_=w1_bf[h][:, t * HALF : (t + 1) * HALF]
                )

        ww = {}

        def deal_words(n, tag):
            ww[n] = sb([P, N], U32, "ww%d" % n, tag)
            nc.vector.tensor_copy(
                ww[n][:].rearrange("p (t g i) -> p g t i", t=PACK, i=4),
                ww_raw[n][:].bitcast(U32).rearrange("p (g i t) -> p g t i", t=PACK, i=4),
            )

        ws = sb([P, N], U8, "ws")

        def deal_scales():
            nc.vector.tensor_copy(ws[:].rearrange("p (t m) -> p t m", t=PACK), ws_raw[:].rearrange("p (m t) -> p t m", t=PACK))

        xg = {}

        def gather_x(first, count, tag=None):
            tile = sb([P, count * CH], U32, "xg%d" % first, tag)
            nc.vector.tensor_copy(tile[:], xw[:].bitcast(U32).indirect(offs_t[:, first * 8 : (first + count) * 8]))
            for c in range(count):
                xg[first + c] = tile[:, c * CH : (c + 1) * CH]

        hid = {}

        def layer1(n, c, bank):
            hid[n, c] = psum.tile([P, PACK, CH], F32, name="hid%d%d" % (n, c), tag=bank)
            for t in range(PACK):
                cols = slice(t * P, (t + 1) * P)
                nc.tensor.matmul_mx(
                    out=hid[n, c][:, t, :],
                    lhsT=w_c[n][:, cols].bitcast(FP8X4),
                    lhsT_scale=w_s[n][:, cols],
                    rhs=xg[c].bitcast(FP8X4),
                    rhs_scale=xg_s[:, c * CH : (c + 1) * CH],
                    start=True,
                    stop=True,
                )

        z_bf = {}

        def gelu(n, c, dst):
            z_bf[n, c] = dst
            nc.scalar.activation(
                dst.rearrange("p a (s t) -> p a s t", t=PACK), hid[n, c][:].rearrange("p t (a s) -> p a s t", a=2), ACT.Gelu_apprx_tanh
            )

        def gelu1(c):
            first = (PACK - 1) * S + CH + c % 2 * HALF
            late = q_flat[:, first : first + HALF].bitcast(BF16).rearrange("p (a x) -> p a x", a=2)
            gelu(1, c, late if c < 2 else sb([P, 2, HALF], BF16, "z1_%d" % c)[:])

        nz = {}

        def negate(c, dst):
            nz[c] = dst
            nc.vector.tensor_scalar_mul(dst, z_bf[2, c], -1.0)

        z_c = {}
        z_s = {}

        def quant_z(n, c, tag=None):
            z_c[n, c] = sb([P, CH], U32, "z_c%d%d" % (n, c), tag)[:]
            z_s[n, c] = sb([P, CH], U8, "z_s%d%d" % (n, c))[:]
            src = nz[c] if n == 2 else z_bf[1, c]
            nc.vector.quantize_mx(out=z_c[n, c].bitcast(FP8X4), scales=z_s[n, c], in_=src.rearrange("p a x -> p (a x)"))

        def quant_pair(first, src, tag):
            codes = sb([P, 2 * CH], U32, "z_pair_c%d" % first, tag)
            scales = sb([P, 2 * CH], U8, "z_pair_s%d" % first)
            nc.vector.quantize_mx(out=codes[:].bitcast(FP8X4), scales=scales[:], in_=src.rearrange("p c a x -> p (c a x)"))
            for i in range(2):
                z_c[2, first + i] = codes[:, i * CH : (i + 1) * CH]
                z_s[2, first + i] = scales[:, i * CH : (i + 1) * CH]

        def passes2(banks, n, c, opens, closes, lone):
            per = PACK // len(banks)
            for t in range(PACK):
                cols = slice(t * P, (t + 1) * P)
                nc.tensor.matmul_mx(
                    out=banks[t // per][:, t % per, :],
                    lhsT=ww[n][:, cols].bitcast(FP8X4),
                    lhsT_scale=ws[4 * n : P, cols],
                    rhs=z_c[n, c].bitcast(FP8X4),
                    rhs_scale=z_s[n, c],
                    start=lone or (opens and t % per == 0),
                    stop=lone or (closes and t % per == per - 1),
                )

        diff = {}
        nb = {}

        def diff_b(c, banks):
            diff[c] = [psum.tile([P, PACK // len(banks), CH], F32, name="diff%d%s" % (c, b), tag=b) for b in banks]
            passes2(diff[c], 2, c, True, False, False)

        def diff_a(c):
            passes2(diff[c], 1, c, False, True, False)

        def minus_b(c, bank):
            nb[c] = psum.tile([P, PACK, CH], F32, name="nb%d" % c, tag=bank)
            passes2([nb[c]], 2, c, False, False, True)

        o_c = sb([P, S], I32, "o_c")
        o_s = sb([P, S], U8, "o_s")
        out_rows = out_0.rearrange("(p t) s -> p t s", t=PACK)
        o1 = out_1[0].rearrange("p n t -> p (n t)").bitcast(I32)
        prod = {}
        y = {}
        y_bf = [sb([P, 2 * CH * PACK], BF16, "y_bf%d" % h) for h in range(2)]

        def mul(c):
            prod[c] = sb([P, PACK, CH], F32, "prod%d" % c)
            per = PACK // len(diff[c])
            for i, bank in enumerate(diff[c]):
                ts = slice(i * per, (i + 1) * per)
                nc.vector.tensor_tensor(prod[c][:, ts, :], bank[:], q[:, ts, c * CH : (c + 1) * CH], ALU.mult)

        def sub(c):
            y[c] = sb([P, PACK, CH], F32, "y%d" % c, "z1_3" if c == POOL_CHUNK else None)
            if c == POOL_CHUNK:
                nc.gpsimd.tensor_tensor(y[c][:], prod[c][:], nb_sb, ALU.subtract)
            else:
                nc.vector.tensor_tensor(y[c][:], prod[c][:], nb[c][:], ALU.subtract)
            nc.sync.dma_start(out_rows[:, :, c * CH : (c + 1) * CH], y[c][:])

        def round_y(on_vector, c, first, last):
            dst = y_bf[c // 2][:, c % 2 * CH * PACK : (c % 2 + 1) * CH * PACK].rearrange("p (g i t) -> p g t i", i=4, t=PACK)
            src = y[c][:].rearrange("p t (g i) -> p g t i", i=4)
            if on_vector:
                nc.vector.tensor_copy(dst[:, first:last], src[:, first:last])
            else:
                nc.scalar.copy(dst[:, first:last], src[:, first:last])

        def quant_y(first, last):
            cols = slice(first * CH, last * CH)
            base = first // 2 * 2
            nc.vector.quantize_mx(
                out=o_c[:, cols].bitcast(FP8X4), scales=o_s[:, cols], in_=y_bf[first // 2][:, (first - base) * CH * PACK : (last - base) * CH * PACK]
            )

        load_mix(0)
        nc.sync.dma_start(task_t[:], task)
        load_mix(1)
        nc.sync.dma_start(offs_t[:], offs)
        nc.sync.dma_start(xs[0:P:8, :].bitcast(I32), x_scales[0].bitcast(I32))
        load_ws(2, (0, 1))
        nc.sync.dma_start(w_raw[2][:], w_rows[2])
        load_ws(2, (2, 3))
        load_ws(1, range(4))
        nc.sync.dma_start(xw[:], x_words[0].rearrange("p n t -> p (n t)").bitcast(I32))

        gather_plane(True, 0)
        gather_plane(False, 1)
        nc.vector.tensor_copy(xg_rows[:], xs[:].indirect(offs_t[:]))
        for r in range(4):
            nc.sync.dma_start(xg_s[r:P:32, :].bitcast(I32), xg_rows[8 * r : P : 32, :].bitcast(I32))
        load_mix(2)
        nc.sync.dma_start(w_raw[1][:], w_rows[1])
        load_mix(3)
        load_ww(2)
        load_ww(1)

        round_w(False, 2, w2_bf, 0, W2_SPLIT, P)
        round_w(True, 2, w2_bf, 0, 0, W2_SPLIT)
        quant_w2(0)
        quant_w2(1)
        deal_scales()
        gather_x(0, 1)
        gather_x(1, 1)
        gather_x(2, 2)
        gather_plane(True, 2)
        for c in range(2):
            layer1(2, c, "AB"[c])
            gelu(2, c, sb([P, 2, HALF], BF16, "z2_%d" % c)[:])
        negate(0, sb([P, 2, HALF], BF16, "nz0")[:])
        layer1(2, 2, "A")
        layer1(2, 3, "B")

        round_w(False, 1, w1_bf[1], 64, W_SPLIT, P)
        round_w(True, 1, w1_bf[0], 0, 0, 64)
        round_w(True, 1, w1_bf[1], 64, 64, W_SPLIT)
        quant_w1(0)
        quant_w1(1)
        for c in range(NCH):
            layer1(1, c, "CDEF"[c])
        gather_q(False, 3, 0, 1)
        for c in range(2, NCH):
            gelu(2, c, w_raw[1][:, 2 * c - 4 : 2 * c - 2, H - CH :].bitcast(BF16))
        nz_all = sb([P, NCH, 2, HALF], BF16, "nz_all", "w1_bf0")
        negate(1, nz_all[:, 1])
        quant_z(2, 0, "w1_bf1")
        deal_words(2, None)
        quant_z(2, 1)
        deal_words(1, None)
        diff_b(0, "GA")
        gelu1(0)
        quant_z(1, 0)
        diff_a(0)
        diff_b(1, "H")
        gelu1(1)
        quant_z(1, 1)
        diff_a(1)
        minus_b(1, "D")
        minus_b(0, "E")
        negate(2, nz_all[:, 2])
        negate(3, nz_all[:, 3])
        quant_pair(2, nz_all[:, 2:], None)
        gelu1(2)
        gather_q(False, 3, 1, 1)
        gelu1(3)
        nb_sb = sb([P, PACK, CH], F32, "nb_sb")[:]
        nc.scalar.copy(nb_sb, nb[1][:])
        gather_q(False, 3, 2, 1)

        mul(0)
        quant_z(1, 2)
        gather_q(False, 3, 3, 1)
        diff_b(2, "F")
        diff_a(2)
        mul(1)
        quant_z(1, 3)
        diff_b(3, "A")
        diff_a(3)
        sub(0)
        sub(1)
        round_y(False, 0, 0, 32)
        round_y(False, 1, 0, 32)
        minus_b(2, "E")
        mul(2)
        minus_b(3, "F")
        mul(3)
        sub(2)
        round_y(False, 2, 0, 32)
        sub(3)
        quant_y(0, 2)
        nc.sync.dma_start(o1[:, :HALF], o_c[:, :HALF])
        round_y(False, 3, 0, 16)
        round_y(True, 3, 16, 32)
        quant_y(2, 3)
        quant_y(3, 4)
        nc.sync.dma_start(o1[:, HALF:], o_c[:, HALF:])
        for r in range(4):
            eng = nc.scalar if r % 2 else nc.sync
            eng.dma_start(out_2[0, 4 * r : 4 * r + 4, :].bitcast(I32), o_s[32 * r : 32 * r + 4, :].bitcast(I32))
